import numpy as np
import ml_dtypes


def mxq(x, axis, fmt="e4m3"):
    dtype, down = {"e4m3": (ml_dtypes.float8_e4m3fn, 7), "e5m2": (ml_dtypes.float8_e5m2, 14)}[fmt]
    v = np.moveaxis(np.asarray(x, np.float32).astype(ml_dtypes.bfloat16).astype(np.float64), axis, -1)
    blocks = v.reshape(v.shape[:-1] + (-1, 32))
    amax = np.abs(blocks).max(-1, keepdims=True)
    byte = np.maximum(np.where(amax > 0, np.frexp(amax)[1] - 1 + 127, 0) - down, 1)
    scale = np.exp2(byte - 127.0)
    codes = (blocks / scale).astype(np.float32).astype(dtype).astype(np.float64)
    return np.moveaxis((codes * scale).reshape(v.shape), -1, axis)


WIDE = False


def mx_kscale(k):
    if not WIDE:
        return np.ones(k)
    levels = np.array([10, -10, 5, -5, 0])
    if k % 512:
        return np.exp2(np.random.permutation(np.resize(levels, k // 32))).repeat(32)
    a = np.empty((k // 512, 16))
    for p in range(k // 512):
        a[p, :8] = np.random.permutation(np.resize(levels, 8))
        for g in range(8):
            far = levels[np.abs(levels - a[p, g]) >= 10]
            a[p, g + 8] = far[np.random.randint(len(far))]
    return np.exp2(a.ravel()).repeat(32)


def f64(x):
    return np.asarray(x).astype(np.float64)


def striped(idx):
    return np.tile(idx.reshape(-1, 16).T, (8, 1)).astype(np.uint16)


def unstriped(offs):
    return offs[:16].T.reshape(-1).astype(np.int64)


def relu(v):
    return np.maximum(v, 0.0)

def planes(y):
    n, m = y.shape
    v = y.astype(np.float32).astype(ml_dtypes.bfloat16).astype(np.float64).reshape(n // 32, 32, m)
    top = np.abs(v).max(1)
    byte = np.clip(np.where(top > 0, np.frexp(top)[1] - 1 + 127 - 7, 1), 1, 254)
    codes = (v * np.exp2(127.0 - byte)[:, None, :]).reshape(n, m).astype(np.float32).astype(ml_dtypes.float8_e4m3fn).view(np.uint8)
    words = codes.reshape(n // 512, 128, 4, m).transpose(0, 1, 3, 2)
    return np.ascontiguousarray(words), np.ascontiguousarray(byte.astype(np.uint8).reshape(n // 512, 16, m))


K, T, S, V, H = 512, 1024, 512, 256, 512


def setup_inputs():
    n = np.random.standard_normal
    s = mx_kscale(K)[:, None]
    u = mx_kscale(H)
    return {
        "xT": (n((K, T)) * s).astype(np.float32),
        "w1": (n((K, H)) / np.sqrt(K) / s * u).astype(np.float32),
        "w2": (n((H, H)) / np.sqrt(2 * H) / u[:, None]).astype(np.float32),
        "w3": (n((H, H)) / np.sqrt(2 * H) / u[:, None]).astype(np.float32),
        "offs": striped(np.random.permutation(T)[:S]),
        "cen": striped(np.random.permutation(S)[:V]),
        "pos1": striped(np.random.permutation(S)[:V]),
        "pos2": striped(np.random.permutation(S)[:V]),
        "pos3": striped(np.random.permutation(S)[:V]),
        "pos4": striped(np.random.permutation(S)[:V]),
    }


def reference(xT, w1, w2, w3, offs, cen, pos1, pos2, pos3, pos4):
    xq = mxq(f64(xT)[:, unstriped(offs)], 0, "e4m3")
    h = relu(mxq(f64(w1), 0, "e4m3").T @ xq)
    g = h[:, unstriped(cen)]
    z = (h[:, unstriped(pos1)] + h[:, unstriped(pos2)] + h[:, unstriped(pos3)] + h[:, unstriped(pos4)]) / 4
    out_0 = mxq(f64(w2), 0, "e4m3").T @ mxq(g, 0, "e4m3") + mxq(f64(w3), 0, "e4m3").T @ mxq(z, 0, "e4m3")
    return (out_0,) + planes(out_0)

@@ -1,0 +1,219 @@
+from contextlib import ExitStack
+
+import concourse.mybir as mybir
+
+K, T, S, V, H = 512, 1024, 512, 256, 512
+FLOPS = 2 * K * H * S + 2 * 2 * H * H * V
+
+F32 = mybir.dt.float32
+BF16 = mybir.dt.bfloat16
+I32 = mybir.dt.int32
+U32 = mybir.dt.uint32
+U16 = mybir.dt.uint16
+U8 = mybir.dt.uint8
+FP8X4 = mybir.dt.float8_e4m3fn_x4
+ADD = mybir.AluOpType.add
+COPY = mybir.ActivationFunctionType.Copy
+RELU = mybir.ActivationFunctionType.Relu
+
+P = 128
+PACK = 4
+HS = S // 2
+HV = V // 2
+
+
+def tile_picked_sagecat_mean_lo_kernel(
+    tc, xT, w1, w2, w3, offs, cen, pos1, pos2, pos3, pos4, out_0, out_1, out_2
+):
+    nc = tc.nc
+
+    def woven(ap):
+        return ap.rearrange("p (c i) t -> p c t i", i=4)
+
+    def planes(ap):
+        return ap.rearrange("p t (c i) -> p c t i", i=4)
+
+    def quantize(codes, scales, values):
+        nc.vector.quantize_mx(out=codes.bitcast(FP8X4), scales=scales, in_=values.rearrange("p c t -> p (c t)"))
+
+    def multiply(acc, w_codes, w_scales, a_codes, a_scales, start, stop):
+        nc.tensor.matmul_mx(
+            out=acc,
+            lhsT=w_codes.bitcast(FP8X4),
+            lhsT_scale=w_scales,
+            rhs=a_codes.bitcast(FP8X4),
+            rhs_scale=a_scales,
+            start=start,
+            stop=stop,
+        )
+
+    with ExitStack() as ctx:
+        sb = ctx.enter_context(tc.tile_pool(name="sb", bufs=1))
+        psum = ctx.enter_context(tc.psum_pool(name="psum", bufs=1))
+
+        def sbuf(name, shape, dtype, tag=None):
+            return sb.tile(shape, dtype, name=name, tag=tag or name, align_bytes=64)
+
+        def bank(number, name, shape):
+            return psum.tile(shape, F32, name=name, tag="bank%d" % number)
+
+        offs_sb = sb.tile([P, S // 16], U16, name="offs_sb")
+        nc.sync.dma_start(offs_sb[:], offs)
+        x_rows = xT.rearrange("(p j) n -> p j n", j=PACK)
+        x_raw = [sbuf("x_raw%d" % j, [P, T], F32) for j in range(PACK)]
+        for j in range(PACK):
+            nc.sync.dma_start(x_raw[j][:], x_rows[:, j, :])
+        w1_raw = sbuf("w1_raw", [P, PACK, H], F32)
+        nc.sync.dma_start(w1_raw[:], w1.rearrange("(p j) c -> p j c", j=PACK))
+        lists = []
+        for number, src in enumerate((pos1, pos2, pos3, pos4, cen)):
+            list_sb = sb.tile([P, V // 16], U16, name="list%d" % number)
+            nc.sync.dma_start(list_sb[:], src)
+            lists.append(list_sb)
+        cen_sb = lists[4]
+        w_raw = []
+        for number, w in enumerate((w3, w2)):
+            raw = sbuf("w_raw%d" % number, [P, PACK, H], F32)
+            rows = w.rearrange("(u t b) c -> b u t c", t=PACK, b=4)
+            for b in range(4):
+                nc.sync.dma_start(raw[b:P:4, :, :], rows[b])
+            w_raw.append(raw)
+
+        def half_of(list_sb, half, entries):
+            return list_sb[:, half * entries // 16 : (half + 1) * entries // 16]
+
+        x_codes = sbuf("x_codes", [P, S], U32)
+        x_scales = sbuf("x_scales", [P, S], U8)
+        x_bf = [sbuf("x_bf%d" % a, [P, HS, PACK], BF16) for a in range(2)]
+        x01 = sbuf("x01", [P, 2, S], F32)
+        for j in range(2):
+            nc.vector.tensor_copy(x01[:, j, :], x_raw[j][:].indirect(offs_sb[:]))
+        for a in range(2):
+            nc.scalar.copy(x_bf[a][:, :, 0:2], x01[:, :, a * HS : (a + 1) * HS].rearrange("p j n -> p n j"))
+        x23 = [sbuf("x23_%d" % a, [P, 2, HS], F32) for a in range(2)]
+        for j in range(2):
+            for a in range(2):
+                nc.vector.tensor_copy(x23[a][:, j, :], x_raw[2 + j][:].indirect(half_of(offs_sb, a, HS)))
+        nc.scalar.copy(x_bf[0][:, :, 2:4], x23[0][:].rearrange("p j n -> p n j"))
+        nc.vector.tensor_copy(x_bf[1][:, :, 2:4], x23[1][:].rearrange("p j n -> p n j"))
+        for a in range(2):
+            cols = slice(a * HS, (a + 1) * HS)
+            quantize(x_codes[:, cols], x_scales[:, cols], x_bf[a][:])
+
+        w1_dealt = w1_raw[:].rearrange("p j (u t b) -> p t u j b", t=PACK, b=4)
+        w1_bf = [sbuf("w1_bf%d" % t, [P, P, PACK], BF16) for t in range(PACK)]
+        for t in range(PACK):
+            dst = w1_bf[t][:].rearrange("p (u b) j -> p u j b", b=4)
+            if t % 2 == 0:
+                nc.vector.tensor_copy(dst, w1_dealt[:, t])
+            else:
+                nc.scalar.copy(dst, w1_dealt[:, t])
+        h = [sbuf("h%d" % t, [P, S], F32) for t in range(PACK)]
+        for t in range(PACK):
+            w1_codes = sbuf("w1_codes%d" % t, [P, P], U32)
+            w1_scales = sbuf("w1_scales%d" % t, [P, P], U8)
+            quantize(w1_codes[:], w1_scales[:], w1_bf[t][:])
+            if t == 0:
+                for a in range(2):
+                    cols = slice(a * HS, (a + 1) * HS)
+                    acc = bank(a, "h0_acc%d" % a, [P, HS])
+                    multiply(acc[:], w1_codes[:], w1_scales[:], x_codes[:, cols], x_scales[:, cols], True, True)
+                    if a == 0:
+                        nc.scalar.activation(h[0][:, cols], acc[:], RELU)
+                    else:
+                        nc.vector.tensor_scalar_max(h[0][:, cols], acc[:], 0.0)
+            else:
+                acc = bank(1 + t, "h_acc%d" % t, [P, S])
+                multiply(acc[:], w1_codes[:], w1_scales[:], x_codes[:], x_scales[:], True, True)
+                nc.scalar.activation(h[t][:], acc[:], RELU)
+
+        w_codes, w_scales = [], []
+        for number in range(2):
+            w_bf = sbuf("w_bf%d" % number, [P, H, PACK], BF16)
+            src = w_raw[number][:].rearrange("p j (m t) -> p m j t", t=PACK)
+            dst = w_bf[:].rearrange("p (t m) j -> p m j t", t=PACK)
+            for q in range(4):
+                nc.scalar.copy(dst[:, 32 * q : 32 * (q + 1)], src[:, 32 * q : 32 * (q + 1)])
+            codes = sbuf("w_codes%d" % number, [P, H], U32)
+            scales = sbuf("w_scales%d" % number, [P, H], U8)
+            quantize(codes[:], scales[:], w_bf[:])
+            w_codes.append(codes)
+            w_scales.append(scales)
+
+        sum2 = []
+        for t in range(PACK):
+            sum1 = sbuf("sum1_%d" % t, [P, V], F32)
+            nc.vector.tensor_copy(sum1[:], h[t][:].indirect(lists[0][:]))
+            both = sbuf("sum2_%d" % t, [P, V], F32)
+            nc.vector.tensor_tensor(both[:], h[t][:].indirect(lists[1][:]), sum1[:], ADD)
+            sum2.append(both)
+
+        y_codes = sbuf("y_codes", [P, V], U32)
+        y_scales = sbuf("y_scales", [P, V], U8)
+        out_rows = out_0.rearrange("(p t) v -> p t v", t=PACK)
+        out_words = out_1[0].rearrange("p c r -> p (c r)").bitcast(I32)
+
+        for a in range(2):
+            cols = slice(a * HV, (a + 1) * HV)
+            if a == 0:
+                sum3 = [sbuf("sum3_%d" % t, [P, HV], F32)[:] for t in range(PACK)]
+            else:
+                low = sbuf("sum3_low", [P, 2, HV], F32, tag="w_bf1")
+                high = sbuf("sum3_high", [P, 2, HV], F32, tag="sum3_2")
+                sum3 = [low[:, 0, :], low[:, 1, :], high[:, 0, :], high[:, 1, :]]
+            if a == 0:
+                g_bf = sbuf("g_bf0", [P, HV, PACK], BF16, tag="w_raw0")
+                g_raw = sbuf("g_raw", [P, PACK, HV], F32)
+                for t in range(PACK):
+                    nc.vector.tensor_copy(g_raw[:, t, :], h[t][:].indirect(half_of(cen_sb, a, HV)))
+            sum4 = sbuf("sum4_%d" % a, [P, PACK, HV], F32, tag="w_raw1" if a == 1 else None)
+            for t in range(PACK):
+                nc.vector.tensor_tensor(sum3[t], h[t][:].indirect(half_of(lists[2], a, HV)), sum2[t][:, cols], ADD)
+            for t in range(PACK):
+                nc.vector.tensor_tensor(sum4[:, t, :], h[t][:].indirect(half_of(lists[3], a, HV)), sum3[t], ADD)
+            z_bf = sbuf("z_bf%d" % a, [P, HV, PACK], BF16, tag="w_raw1" if a == 0 else None)
+            nc.scalar.activation(woven(z_bf[:]), planes(sum4[:]), COPY, scale=0.25)
+            z_codes = sbuf("z_codes%d" % a, [P, HV], U32)
+            z_scales = sbuf("z_scales%d" % a, [P, HV], U8)
+            quantize(z_codes[:], z_scales[:], z_bf[:])
+
+            g_codes = sbuf("g_codes%d" % a, [P, HV], U32)
+            g_scales = sbuf("g_scales%d" % a, [P, HV], U8)
+            if a == 0:
+                nc.scalar.copy(woven(g_bf[:]), planes(g_raw[:]))
+            else:
+                g_bf = sbuf("g_bf1", [P, HV, PACK], BF16, tag="w_bf1")
+                for t in range(PACK):
+                    nc.vector.tensor_copy(g_bf[:, :, t], h[t][:].indirect(half_of(cen_sb, a, HV)))
+            quantize(g_codes[:], g_scales[:], g_bf[:])
+
+            y = sbuf("y%d" % a, [P, PACK, HV], F32)
+            y_bf = sbuf("y_bf%d" % a, [P, HV, PACK], BF16)
+            if a == 0:
+                whole = bank(5, "y_acc", [P, PACK, HV])
+                accs = [whole[:, t, :] for t in range(PACK)]
+                for t in range(PACK):
+                    m = slice(t * P, (t + 1) * P)
+                    multiply(accs[t], w_codes[0][:, m], w_scales[0][:, m], z_codes[:], z_scales[:], True, False)
+                    multiply(accs[t], w_codes[1][:, m], w_scales[1][:, m], g_codes[:], g_scales[:], False, True)
+                nc.scalar.copy(woven(y_bf[:]), planes(whole[:]))
+                nc.scalar.copy(y[:], whole[:])
+            else:
+                accs = [bank((6 + t) % 8, "y_acc%d" % t, [P, HV])[:] for t in range(PACK)]
+                for t in range(PACK):
+                    m = slice(t * P, (t + 1) * P)
+                    multiply(accs[t], w_codes[0][:, m], w_scales[0][:, m], z_codes[:], z_scales[:], True, False)
+                for t in range(PACK):
+                    m = slice(t * P, (t + 1) * P)
+                    multiply(accs[t], w_codes[1][:, m], w_scales[1][:, m], g_codes[:], g_scales[:], False, True)
+                    if t % 2 == 0:
+                        nc.scalar.copy(y[:, t, :], accs[t])
+                    else:
+                        nc.vector.tensor_copy(y[:, t, :], accs[t])
+                nc.vector.tensor_copy(woven(y_bf[:]), planes(y[:]))
+            nc.sync.dma_start(out_rows[:, :, cols], y[:])
+            quantize(y_codes[:, cols], y_scales[:, cols], y_bf[:])
+            nc.sync.dma_start(out_words[:, cols], y_codes[:, cols].bitcast(I32))
+        for q in range(4):
+            queue = nc.scalar if q % 2 == 0 else nc.sync
+            queue.dma_start(out_2[0, 4 * q : 4 * q + 4, :].bitcast(I32), y_scales[32 * q : 32 * q + 4, :].bitcast(I32))

@@ -58,11 +58,12 @@ def tile_picked_sagecat_mean_lo_kernel(
             return psum.tile(shape, F32, name=name, tag="bank%d" % number)
 
         offs_sb = sb.tile([P, S // 16], U16, name="offs_sb")
-        nc.sync.dma_start(offs_sb[:], offs)
         x_rows = xT.rearrange("(p j) n -> p j n", j=PACK)
         x_raw = [sbuf("x_raw%d" % j, [P, T], F32) for j in range(PACK)]
         for j in range(PACK):
             nc.sync.dma_start(x_raw[j][:], x_rows[:, j, :])
+            if j == 0:
+                nc.sync.dma_start(offs_sb[:], offs)
         w1_raw = sbuf("w1_raw", [P, PACK, H], F32)
         nc.sync.dma_start(w1_raw[:], w1.rearrange("(p j) c -> p j c", j=PACK))
         lists = []
@@ -90,25 +91,23 @@ def tile_picked_sagecat_mean_lo_kernel(
             nc.vector.tensor_copy(x01[:, j, :], x_raw[j][:].indirect(offs_sb[:]))
         for a in range(2):
             nc.scalar.copy(x_bf[a][:, :, 0:2], x01[:, :, a * HS : (a + 1) * HS].rearrange("p j n -> p n j"))
-        x23 = [sbuf("x23_%d" % a, [P, 2, HS], F32) for a in range(2)]
-        for j in range(2):
-            for a in range(2):
-                nc.vector.tensor_copy(x23[a][:, j, :], x_raw[2 + j][:].indirect(half_of(offs_sb, a, HS)))
-        nc.scalar.copy(x_bf[0][:, :, 2:4], x23[0][:].rearrange("p j n -> p n j"))
-        nc.vector.tensor_copy(x_bf[1][:, :, 2:4], x23[1][:].rearrange("p j n -> p n j"))
+        x23 = sbuf("x23", [P, 2, S], F32)
+        nc.vector.tensor_copy(x23[:, 0, :], x_raw[2][:].indirect(offs_sb[:]))
+        for a in range(2):
+            nc.vector.tensor_copy(x23[:, 1, a * HS : (a + 1) * HS], x_raw[3][:].indirect(half_of(offs_sb, a, HS)))
+        nc.scalar.copy(x_bf[0][:, :, 2:4], x23[:, :, 0:HS].rearrange("p j n -> p n j"))
+        nc.vector.tensor_copy(x_bf[1][:, :, 2:4], x23[:, :, HS:S].rearrange("p j n -> p n j"))
         for a in range(2):
             cols = slice(a * HS, (a + 1) * HS)
             quantize(x_codes[:, cols], x_scales[:, cols], x_bf[a][:])
 
         w1_dealt = w1_raw[:].rearrange("p j (u t b) -> p t u j b", t=PACK, b=4)
-        w1_bf = [sbuf("w1_bf%d" % t, [P, P, PACK], BF16) for t in range(PACK)]
-        for t in range(PACK):
-            dst = w1_bf[t][:].rearrange("p (u b) j -> p u j b", b=4)
-            if t % 2 == 0:
-                nc.vector.tensor_copy(dst, w1_dealt[:, t])
-            else:
-                nc.scalar.copy(dst, w1_dealt[:, t])
         h = [sbuf("h%d" % t, [P, S], F32) for t in range(PACK)]
+        w1_bf = []
+        for t in range(2):
+            rounded = sbuf("w1_bf%d" % t, [P, P, PACK], BF16)
+            nc.scalar.copy(rounded[:].rearrange("p (u b) j -> p u j b", b=4), w1_dealt[:, t])
+            w1_bf.append(rounded)
         for t in range(PACK):
             w1_codes = sbuf("w1_codes%d" % t, [P, P], U32)
             w1_scales = sbuf("w1_scales%d" % t, [P, P], U8)
@@ -118,102 +117,111 @@ def tile_picked_sagecat_mean_lo_kernel(
                     cols = slice(a * HS, (a + 1) * HS)
                     acc = bank(a, "h0_acc%d" % a, [P, HS])
                     multiply(acc[:], w1_codes[:], w1_scales[:], x_codes[:, cols], x_scales[:, cols], True, True)
-                    if a == 0:
-                        nc.scalar.activation(h[0][:, cols], acc[:], RELU)
-                    else:
-                        nc.vector.tensor_scalar_max(h[0][:, cols], acc[:], 0.0)
+                    nc.scalar.activation(h[0][:, cols], acc[:], RELU)
             else:
                 acc = bank(1 + t, "h_acc%d" % t, [P, S])
                 multiply(acc[:], w1_codes[:], w1_scales[:], x_codes[:], x_scales[:], True, True)
                 nc.scalar.activation(h[t][:], acc[:], RELU)
+            if t < 2:
+                rounded = sbuf("w1_bf%d" % (t + 2), [P, P, PACK], BF16, tag="w1_bf%d" % t)
+                nc.vector.tensor_copy(rounded[:].rearrange("p (u b) j -> p u j b", b=4), w1_dealt[:, t + 2])
+                w1_bf.append(rounded)
 
-        w_codes, w_scales = [], []
+        w_bf = sbuf("w_bf", [P, 2, H, PACK], BF16)
         for number in range(2):
-            w_bf = sbuf("w_bf%d" % number, [P, H, PACK], BF16)
             src = w_raw[number][:].rearrange("p j (m t) -> p m j t", t=PACK)
-            dst = w_bf[:].rearrange("p (t m) j -> p m j t", t=PACK)
+            dst = w_bf[:, number].rearrange("p (t m) j -> p m j t", t=PACK)
             for q in range(4):
                 nc.scalar.copy(dst[:, 32 * q : 32 * (q + 1)], src[:, 32 * q : 32 * (q + 1)])
-            codes = sbuf("w_codes%d" % number, [P, H], U32)
-            scales = sbuf("w_scales%d" % number, [P, H], U8)
-            quantize(codes[:], scales[:], w_bf[:])
-            w_codes.append(codes)
-            w_scales.append(scales)
+        w_codes = sbuf("w_codes", [P, 2 * H], U32)
+        w_scales = sbuf("w_scales", [P, 2 * H], U8)
+        quantize(w_codes[:], w_scales[:], w_bf[:].rearrange("p n c t -> p (n c) t"))
 
-        sum2 = []
+        def second(acc, number, t, codes, scales):
+            m = slice(number * H + t * P, number * H + (t + 1) * P)
+            multiply(acc, w_codes[:, m], w_scales[:, m], codes, scales, number == 0, number == 1)
+
+        sum1 = sbuf("sum1", [P, PACK, V], F32)
+        g_raw = sbuf("g_raw", [P, PACK, HV], F32)
         for t in range(PACK):
-            sum1 = sbuf("sum1_%d" % t, [P, V], F32)
-            nc.vector.tensor_copy(sum1[:], h[t][:].indirect(lists[0][:]))
-            both = sbuf("sum2_%d" % t, [P, V], F32)
-            nc.vector.tensor_tensor(both[:], h[t][:].indirect(lists[1][:]), sum1[:], ADD)
-            sum2.append(both)
+            nc.vector.tensor_copy(sum1[:, t, :], h[t][:].indirect(lists[0][:]))
+            nc.vector.tensor_copy(g_raw[:, t, :], h[t][:].indirect(half_of(cen_sb, 0, HV)))
+        sum2 = sbuf("sum2", [P, PACK, V], F32, tag="x_codes")
+        for t in range(PACK):
+            nc.vector.tensor_tensor(sum2[:, t, :], h[t][:].indirect(lists[1][:]), sum1[:, t, :], ADD)
+        sum3 = [sbuf("sum3_%d" % u, [P, 2, V], F32) for u in range(2)]
+        for t in range(PACK):
+            nc.vector.tensor_tensor(sum3[t // 2][:, t % 2, :], h[t][:].indirect(lists[2][:]), sum2[:, t, :], ADD)
 
         y_codes = sbuf("y_codes", [P, V], U32)
         y_scales = sbuf("y_scales", [P, V], U8)
         out_rows = out_0.rearrange("(p t) v -> p t v", t=PACK)
         out_words = out_1[0].rearrange("p c r -> p (c r)").bitcast(I32)
 
-        for a in range(2):
+        def last_sums(name, a, tag):
+            sum4 = sbuf(name, [P, PACK, HV], F32, tag=tag)
+            for t in range(PACK):
+                earlier = sum3[t // 2][:, t % 2, a * HV : (a + 1) * HV]
+                nc.vector.tensor_tensor(sum4[:, t, :], h[t][:].indirect(half_of(lists[3], a, HV)), earlier, ADD)
+            return sum4
+
+        def hand_out(a, y, y_bf):
             cols = slice(a * HV, (a + 1) * HV)
-            if a == 0:
-                sum3 = [sbuf("sum3_%d" % t, [P, HV], F32)[:] for t in range(PACK)]
-            else:
-                low = sbuf("sum3_low", [P, 2, HV], F32, tag="w_bf1")
-                high = sbuf("sum3_high", [P, 2, HV], F32, tag="sum3_2")
-                sum3 = [low[:, 0, :], low[:, 1, :], high[:, 0, :], high[:, 1, :]]
-            if a == 0:
-                g_bf = sbuf("g_bf0", [P, HV, PACK], BF16, tag="w_raw0")
-                g_raw = sbuf("g_raw", [P, PACK, HV], F32)
-                for t in range(PACK):
-                    nc.vector.tensor_copy(g_raw[:, t, :], h[t][:].indirect(half_of(cen_sb, a, HV)))
-            sum4 = sbuf("sum4_%d" % a, [P, PACK, HV], F32, tag="w_raw1" if a == 1 else None)
-            for t in range(PACK):
-                nc.vector.tensor_tensor(sum3[t], h[t][:].indirect(half_of(lists[2], a, HV)), sum2[t][:, cols], ADD)
-            for t in range(PACK):
-                nc.vector.tensor_tensor(sum4[:, t, :], h[t][:].indirect(half_of(lists[3], a, HV)), sum3[t], ADD)
-            z_bf = sbuf("z_bf%d" % a, [P, HV, PACK], BF16, tag="w_raw1" if a == 0 else None)
-            nc.scalar.activation(woven(z_bf[:]), planes(sum4[:]), COPY, scale=0.25)
-            z_codes = sbuf("z_codes%d" % a, [P, HV], U32)
-            z_scales = sbuf("z_scales%d" % a, [P, HV], U8)
-            quantize(z_codes[:], z_scales[:], z_bf[:])
-
-            g_codes = sbuf("g_codes%d" % a, [P, HV], U32)
-            g_scales = sbuf("g_scales%d" % a, [P, HV], U8)
-            if a == 0:
-                nc.scalar.copy(woven(g_bf[:]), planes(g_raw[:]))
-            else:
-                g_bf = sbuf("g_bf1", [P, HV, PACK], BF16, tag="w_bf1")
-                for t in range(PACK):
-                    nc.vector.tensor_copy(g_bf[:, :, t], h[t][:].indirect(half_of(cen_sb, a, HV)))
-            quantize(g_codes[:], g_scales[:], g_bf[:])
-
-            y = sbuf("y%d" % a, [P, PACK, HV], F32)
-            y_bf = sbuf("y_bf%d" % a, [P, HV, PACK], BF16)
-            if a == 0:
-                whole = bank(5, "y_acc", [P, PACK, HV])
-                accs = [whole[:, t, :] for t in range(PACK)]
-                for t in range(PACK):
-                    m = slice(t * P, (t + 1) * P)
-                    multiply(accs[t], w_codes[0][:, m], w_scales[0][:, m], z_codes[:], z_scales[:], True, False)
-                    multiply(accs[t], w_codes[1][:, m], w_scales[1][:, m], g_codes[:], g_scales[:], False, True)
-                nc.scalar.copy(woven(y_bf[:]), planes(whole[:]))
-                nc.scalar.copy(y[:], whole[:])
-            else:
-                accs = [bank((6 + t) % 8, "y_acc%d" % t, [P, HV])[:] for t in range(PACK)]
-                for t in range(PACK):
-                    m = slice(t * P, (t + 1) * P)
-                    multiply(accs[t], w_codes[0][:, m], w_scales[0][:, m], z_codes[:], z_scales[:], True, False)
-                for t in range(PACK):
-                    m = slice(t * P, (t + 1) * P)
-                    multiply(accs[t], w_codes[1][:, m], w_scales[1][:, m], g_codes[:], g_scales[:], False, True)
-                    if t % 2 == 0:
-                        nc.scalar.copy(y[:, t, :], accs[t])
-                    else:
-                        nc.vector.tensor_copy(y[:, t, :], accs[t])
-                nc.vector.tensor_copy(woven(y_bf[:]), planes(y[:]))
             nc.sync.dma_start(out_rows[:, :, cols], y[:])
             quantize(y_codes[:, cols], y_scales[:, cols], y_bf[:])
             nc.sync.dma_start(out_words[:, cols], y_codes[:, cols].bitcast(I32))
+
+        sum4 = last_sums("sum4_0", 0, None)
+        zg_bf = sbuf("zg_bf", [P, 2, HV, PACK], BF16, tag="w_raw1")
+        nc.scalar.copy(woven(zg_bf[:, 1]), planes(g_raw[:]))
+        nc.scalar.activation(woven(zg_bf[:, 0]), planes(sum4[:]), COPY, scale=0.25)
+        zg_codes = sbuf("zg_codes", [P, V], U32)
+        zg_scales = sbuf("zg_scales", [P, V], U8)
+        quantize(zg_codes[:], zg_scales[:], zg_bf[:].rearrange("p n c t -> p (n c) t"))
+        whole = bank(5, "y_acc", [P, PACK, HV])
+        for t in range(PACK):
+            for number in range(2):
+                cols = slice(number * HV, (number + 1) * HV)
+                second(whole[:, t, :], number, t, zg_codes[:, cols], zg_scales[:, cols])
+
+        sum4 = last_sums("sum4_1", 1, "w_raw1")
+        z_bf = sbuf("z_bf", [P, HV, PACK], BF16)
+        nc.scalar.activation(woven(z_bf[:]), planes(sum4[:]), COPY, scale=0.25)
+        z_codes = sbuf("z_codes", [P, HV], U32)
+        z_scales = sbuf("z_scales", [P, HV], U8)
+        quantize(z_codes[:], z_scales[:], z_bf[:])
+        g_last = sbuf("g_last", [P, 4 * HV], F32, tag="sum3_0")
+        g_pair = g_last[:, 0 : 2 * HV].rearrange("p (t v) -> p t v", t=2)
+        g_bf = g_last[:, 2 * HV : 4 * HV].bitcast(BF16).rearrange("p (v t) -> p v t", t=PACK)
+        for t in range(2):
+            nc.vector.tensor_copy(g_pair[:, t, :], h[t][:].indirect(half_of(cen_sb, 1, HV)))
+        nc.scalar.copy(g_bf[:, :, 0:2], g_pair.rearrange("p t v -> p v t"))
+        for t in range(2, PACK):
+            nc.vector.tensor_copy(g_bf[:, :, t], h[t][:].indirect(half_of(cen_sb, 1, HV)))
+        g_codes = sbuf("g_codes", [P, HV], U32)
+        g_scales = sbuf("g_scales", [P, HV], U8)
+        quantize(g_codes[:], g_scales[:], g_bf)
+
+        y = sbuf("y0", [P, PACK, HV], F32)
+        y_bf = sbuf("y_bf0", [P, HV, PACK], BF16)
+        nc.scalar.copy(woven(y_bf[:]), planes(whole[:]))
+        nc.scalar.copy(y[:], whole[:])
+        hand_out(0, y, y_bf)
+
+        y = sbuf("y1", [P, PACK, HV], F32)
+        y_bf = sbuf("y_bf1", [P, HV, PACK], BF16)
+        accs = [bank((6 + t) % 8, "y_acc%d" % t, [P, HV])[:] for t in range(PACK)]
+        for t in range(PACK):
+            second(accs[t], 0, t, z_codes[:], z_scales[:])
+        for t in range(PACK):
+            second(accs[t], 1, t, g_codes[:], g_scales[:])
+            if t % 2 == 0:
+                nc.vector.tensor_copy(y[:, t, :], accs[t])
+            else:
+                nc.scalar.copy(y[:, t, :], accs[t])
+                pair = slice(t - 1, t + 1)
+                nc.vector.tensor_copy(y_bf[:, :, pair], y[:, pair, :].rearrange("p t v -> p v t"))
+        hand_out(1, y, y_bf)
         for q in range(4):
             queue = nc.scalar if q % 2 == 0 else nc.sync
             queue.dma_start(out_2[0, 4 * q : 4 * q + 4, :].bitcast(I32), y_scales[32 * q : 32 * q + 4, :].bitcast(I32))

@@ -169,7 +169,8 @@ def tile_picked_sagecat_mean_lo_kernel(
             cols = slice(a * HV, (a + 1) * HV)
             nc.sync.dma_start(out_rows[:, :, cols], y[:])
             quantize(y_codes[:, cols], y_scales[:, cols], y_bf[:])
-            nc.sync.dma_start(out_words[:, cols], y_codes[:, cols].bitcast(I32))
+            queue = nc.sync if a == 0 else nc.scalar
+            queue.dma_start(out_words[:, cols], y_codes[:, cols].bitcast(I32))
 
         sum4 = last_sums("sum4_0", 0, None)
         zg_bf = sbuf("zg_bf", [P, 2, HV, PACK], BF16, tag="w_raw1")
@@ -223,5 +224,5 @@ def tile_picked_sagecat_mean_lo_kernel(
                 nc.vector.tensor_copy(y_bf[:, :, pair], y[:, pair, :].rearrange("p t v -> p v t"))
         hand_out(1, y, y_bf)
         for q in range(4):
-            queue = nc.scalar if q % 2 == 0 else nc.sync
+            queue = nc.scalar if q == 3 else nc.sync
             queue.dma_start(out_2[0, 4 * q : 4 * q + 4, :].bitcast(I32), y_scales[32 * q : 32 * q + 4, :].bitcast(I32))

@@ -93,10 +93,14 @@ def tile_picked_sagecat_mean_lo_kernel(
             nc.scalar.copy(x_bf[a][:, :, 0:2], x01[:, :, a * HS : (a + 1) * HS].rearrange("p j n -> p n j"))
         x23 = sbuf("x23", [P, 2, S], F32)
         nc.vector.tensor_copy(x23[:, 0, :], x_raw[2][:].indirect(offs_sb[:]))
-        for a in range(2):
-            nc.vector.tensor_copy(x23[:, 1, a * HS : (a + 1) * HS], x_raw[3][:].indirect(half_of(offs_sb, a, HS)))
-        nc.scalar.copy(x_bf[0][:, :, 2:4], x23[:, :, 0:HS].rearrange("p j n -> p n j"))
-        nc.vector.tensor_copy(x_bf[1][:, :, 2:4], x23[:, :, HS:S].rearrange("p j n -> p n j"))
+        for q in range(4):
+            cols = slice(q * P, (q + 1) * P)
+            nc.vector.tensor_copy(x23[:, 1, cols], x_raw[3][:].indirect(offs_sb[:, q * P // 16 : (q + 1) * P // 16]))
+            woven_pair = x_bf[q // 2][:, (q % 2) * P : (q % 2 + 1) * P, 2:4]
+            if q < 2:
+                nc.scalar.copy(woven_pair, x23[:, :, cols].rearrange("p j n -> p n j"))
+            else:
+                nc.vector.tensor_copy(woven_pair, x23[:, :, cols].rearrange("p j n -> p n j"))
         for a in range(2):
             cols = slice(a * HS, (a + 1) * HS)
             quantize(x_codes[:, cols], x_scales[:, cols], x_bf[a][:])
@@ -123,8 +127,9 @@ def tile_picked_sagecat_mean_lo_kernel(
                 multiply(acc[:], w1_codes[:], w1_scales[:], x_codes[:], x_scales[:], True, True)
                 nc.scalar.activation(h[t][:], acc[:], RELU)
             if t < 2:
-                rounded = sbuf("w1_bf%d" % (t + 2), [P, P, PACK], BF16, tag="w1_bf%d" % t)
-                nc.vector.tensor_copy(rounded[:].rearrange("p (u b) j -> p u j b", b=4), w1_dealt[:, t + 2])
+                rounded = sbuf("w1_bf%d" % (t + 2), [P, P, PACK], BF16, tag=("w1_bf0", "w1_codes0")[t])
+                cast = (nc.vector.tensor_copy, nc.scalar.copy)[t]
+                cast(rounded[:].rearrange("p (u b) j -> p u j b", b=4), w1_dealt[:, t + 2])
                 w1_bf.append(rounded)
 
         w_bf = sbuf("w_bf", [P, 2, H, PACK], BF16)
@@ -185,7 +190,10 @@ def tile_picked_sagecat_mean_lo_kernel(
                 cols = slice(number * HV, (number + 1) * HV)
                 second(whole[:, t, :], number, t, zg_codes[:, cols], zg_scales[:, cols])
 
-        sum4 = last_sums("sum4_1", 1, "w_raw1")
+        sum4 = sbuf("sum4_1", [P, PACK, HV], F32, tag="sum4_0")
+        for t in range(PACK):
+            earlier = sum3[t // 2][:, t % 2, HV:V]
+            nc.vector.tensor_tensor(sum4[:, t, :], h[t][:].indirect(half_of(lists[3], 1, HV)), earlier, ADD)
         z_bf = sbuf("z_bf", [P, HV, PACK], BF16)
         nc.scalar.activation(woven(z_bf[:]), planes(sum4[:]), COPY, scale=0.25)
         z_codes = sbuf("z_codes", [P, HV], U32)

@@ -170,12 +170,9 @@ def tile_picked_sagecat_mean_lo_kernel(
                 nc.vector.tensor_tensor(sum4[:, t, :], h[t][:].indirect(half_of(lists[3], a, HV)), earlier, ADD)
             return sum4
 
-        def hand_out(a, y, y_bf):
+        def hand_out(a, y_bf):
             cols = slice(a * HV, (a + 1) * HV)
-            nc.sync.dma_start(out_rows[:, :, cols], y[:])
             quantize(y_codes[:, cols], y_scales[:, cols], y_bf[:])
-            queue = nc.sync if a == 0 else nc.scalar
-            queue.dma_start(out_words[:, cols], y_codes[:, cols].bitcast(I32))
 
         sum4 = last_sums("sum4_0", 0, None)
         zg_bf = sbuf("zg_bf", [P, 2, HV, PACK], BF16, tag="w_raw1")
@@ -215,22 +212,26 @@ def tile_picked_sagecat_mean_lo_kernel(
         y_bf = sbuf("y_bf0", [P, HV, PACK], BF16)
         nc.scalar.copy(woven(y_bf[:]), planes(whole[:]))
         nc.scalar.copy(y[:], whole[:])
-        hand_out(0, y, y_bf)
+        nc.sync.dma_start(out_rows[:, :, 0:HV], y[:])
+        hand_out(0, y_bf)
 
         y = sbuf("y1", [P, PACK, HV], F32)
         y_bf = sbuf("y_bf1", [P, HV, PACK], BF16)
-        accs = [bank((6 + t) % 8, "y_acc%d" % t, [P, HV])[:] for t in range(PACK)]
-        for t in range(PACK):
-            second(accs[t], 0, t, z_codes[:], z_scales[:])
-        for t in range(PACK):
-            second(accs[t], 1, t, g_codes[:], g_scales[:])
-            if t % 2 == 0:
-                nc.vector.tensor_copy(y[:, t, :], accs[t])
-            else:
-                nc.scalar.copy(y[:, t, :], accs[t])
-                pair = slice(t - 1, t + 1)
-                nc.vector.tensor_copy(y_bf[:, :, pair], y[:, pair, :].rearrange("p t v -> p v t"))
-        hand_out(1, y, y_bf)
+        accs = [bank(6 + u, "y_acc%d" % u, [P, 2, HV]) for u in range(2)]
+        for u in range(2):
+            second(accs[u][:, 0, :], 0, 2 * u, z_codes[:], z_scales[:])
+        for u in range(2):
+            second(accs[u][:, 0, :], 1, 2 * u, g_codes[:], g_scales[:])
+            second(accs[u][:, 1, :], 0, 2 * u + 1, z_codes[:], z_scales[:])
+            second(accs[u][:, 1, :], 1, 2 * u + 1, g_codes[:], g_scales[:])
+        nc.vector.tensor_copy(y_bf[:, :, 0:2], accs[0][:].rearrange("p t v -> p v t"))
+        nc.scalar.copy(y_bf[:, :, 2:4], accs[1][:].rearrange("p t v -> p v t"))
+        nc.vector.tensor_copy(y[:, 0:2, :], accs[0][:])
+        nc.sync.dma_start(out_rows[:, 0:2, HV:V], y[:, 0:2, :])
+        nc.scalar.copy(y[:, 2:4, :], accs[1][:])
+        nc.scalar.dma_start(out_rows[:, 2:4, HV:V], y[:, 2:4, :])
+        hand_out(1, y_bf)
+        nc.sync.dma_start(out_words, y_codes[:].bitcast(I32))
         for q in range(4):
-            queue = nc.scalar if q == 3 else nc.sync
+            queue = nc.scalar if q >= 2 else nc.sync
             queue.dma_start(out_2[0, 4 * q : 4 * q + 4, :].bitcast(I32), y_scales[32 * q : 32 * q + 4, :].bitcast(I32))

@@ -217,18 +217,20 @@ def tile_picked_sagecat_mean_lo_kernel(
 
         y = sbuf("y1", [P, PACK, HV], F32)
         y_bf = sbuf("y_bf1", [P, HV, PACK], BF16)
-        accs = [bank(6 + u, "y_acc%d" % u, [P, 2, HV]) for u in range(2)]
-        for u in range(2):
-            second(accs[u][:, 0, :], 0, 2 * u, z_codes[:], z_scales[:])
-        for u in range(2):
-            second(accs[u][:, 0, :], 1, 2 * u, g_codes[:], g_scales[:])
-            second(accs[u][:, 1, :], 0, 2 * u + 1, z_codes[:], z_scales[:])
-            second(accs[u][:, 1, :], 1, 2 * u + 1, g_codes[:], g_scales[:])
-        nc.vector.tensor_copy(y_bf[:, :, 0:2], accs[0][:].rearrange("p t v -> p v t"))
-        nc.scalar.copy(y_bf[:, :, 2:4], accs[1][:].rearrange("p t v -> p v t"))
-        nc.vector.tensor_copy(y[:, 0:2, :], accs[0][:])
+        last_pair = bank(6, "y_acc_pair", [P, 2, HV])
+        accs = [bank(7, "y_acc0", [P, HV])[:], bank(0, "y_acc1", [P, HV])[:], last_pair[:, 0, :], last_pair[:, 1, :]]
+        for t in range(3):
+            second(accs[t], 0, t, z_codes[:], z_scales[:])
+        for t in range(3):
+            second(accs[t], 1, t, g_codes[:], g_scales[:])
+        second(accs[3], 0, 3, z_codes[:], z_scales[:])
+        second(accs[3], 1, 3, g_codes[:], g_scales[:])
+        for t in range(2):
+            nc.scalar.copy(y[:, t, :], accs[t])
         nc.sync.dma_start(out_rows[:, 0:2, HV:V], y[:, 0:2, :])
-        nc.scalar.copy(y[:, 2:4, :], accs[1][:])
+        nc.vector.tensor_copy(y_bf[:, :, 0:2], y[:, 0:2, :].rearrange("p t v -> p v t"))
+        nc.scalar.copy(y_bf[:, :, 2:4], last_pair[:].rearrange("p t v -> p v t"))
+        nc.scalar.copy(y[:, 2:4, :], last_pair[:])
         nc.scalar.dma_start(out_rows[:, 2:4, HV:V], y[:, 2:4, :])
         hand_out(1, y_bf)
         nc.sync.dma_start(out_words, y_codes[:].bitcast(I32))

@@ -187,11 +187,14 @@ def tile_picked_sagecat_mean_lo_kernel(
                 cols = slice(number * HV, (number + 1) * HV)
                 second(whole[:, t, :], number, t, zg_codes[:, cols], zg_scales[:, cols])
 
+        y = sbuf("y0", [P, PACK, HV], F32)
+        nc.scalar.copy(y[:, 0:2, :], whole[:, 0:2, :])
+
         sum4 = sbuf("sum4_1", [P, PACK, HV], F32, tag="sum4_0")
         for t in range(PACK):
             earlier = sum3[t // 2][:, t % 2, HV:V]
             nc.vector.tensor_tensor(sum4[:, t, :], h[t][:].indirect(half_of(lists[3], 1, HV)), earlier, ADD)
-        z_bf = sbuf("z_bf", [P, HV, PACK], BF16)
+        z_bf = sbuf("z_bf", [P, HV, PACK], BF16, tag="zg_scales")
         nc.scalar.activation(woven(z_bf[:]), planes(sum4[:]), COPY, scale=0.25)
         z_codes = sbuf("z_codes", [P, HV], U32)
         z_scales = sbuf("z_scales", [P, HV], U8)
@@ -208,11 +211,10 @@ def tile_picked_sagecat_mean_lo_kernel(
         g_scales = sbuf("g_scales", [P, HV], U8)
         quantize(g_codes[:], g_scales[:], g_bf)
 
-        y = sbuf("y0", [P, PACK, HV], F32)
+        nc.scalar.copy(y[:, 2:4, :], whole[:, 2:4, :])
+        nc.sync.dma_start(out_rows[:, :, 0:HV], y[:])
         y_bf = sbuf("y_bf0", [P, HV, PACK], BF16)
         nc.scalar.copy(woven(y_bf[:]), planes(whole[:]))
-        nc.scalar.copy(y[:], whole[:])
-        nc.sync.dma_start(out_rows[:, :, 0:HV], y[:])
         hand_out(0, y_bf)
 
         y = sbuf("y1", [P, PACK, HV], F32)

@@ -86,21 +86,14 @@ def tile_picked_sagecat_mean_lo_kernel(
         x_codes = sbuf("x_codes", [P, S], U32)
         x_scales = sbuf("x_scales", [P, S], U8)
         x_bf = [sbuf("x_bf%d" % a, [P, HS, PACK], BF16) for a in range(2)]
-        x01 = sbuf("x01", [P, 2, S], F32)
-        for j in range(2):
-            nc.vector.tensor_copy(x01[:, j, :], x_raw[j][:].indirect(offs_sb[:]))
-        for a in range(2):
-            nc.scalar.copy(x_bf[a][:, :, 0:2], x01[:, :, a * HS : (a + 1) * HS].rearrange("p j n -> p n j"))
-        x23 = sbuf("x23", [P, 2, S], F32)
-        nc.vector.tensor_copy(x23[:, 0, :], x_raw[2][:].indirect(offs_sb[:]))
+        x_found = sbuf("x_found", [P, PACK, S], F32)
+        for j in range(PACK - 1):
+            nc.vector.tensor_copy(x_found[:, j, :], x_raw[j][:].indirect(offs_sb[:]))
         for q in range(4):
             cols = slice(q * P, (q + 1) * P)
-            nc.vector.tensor_copy(x23[:, 1, cols], x_raw[3][:].indirect(offs_sb[:, q * P // 16 : (q + 1) * P // 16]))
-            woven_pair = x_bf[q // 2][:, (q % 2) * P : (q % 2 + 1) * P, 2:4]
-            if q < 2:
-                nc.scalar.copy(woven_pair, x23[:, :, cols].rearrange("p j n -> p n j"))
-            else:
-                nc.vector.tensor_copy(woven_pair, x23[:, :, cols].rearrange("p j n -> p n j"))
+            nc.vector.tensor_copy(x_found[:, 3, cols], x_raw[3][:].indirect(offs_sb[:, q * P // 16 : (q + 1) * P // 16]))
+            weave = nc.scalar.copy if q < 2 else nc.vector.tensor_copy
+            weave(woven(x_bf[q // 2][:, (q % 2) * P : (q % 2 + 1) * P, :]), planes(x_found[:, :, cols]))
         for a in range(2):
             cols = slice(a * HS, (a + 1) * HS)
             quantize(x_codes[:, cols], x_scales[:, cols], x_bf[a][:])

@@ -140,10 +140,13 @@ def tile_picked_sagecat_mean_lo_kernel(
             multiply(acc, w_codes[:, m], w_scales[:, m], codes, scales, number == 0, number == 1)
 
         sum1 = sbuf("sum1", [P, PACK, V], F32)
-        g_raw = sbuf("g_raw", [P, PACK, HV], F32)
+        g_raw = sbuf("g_raw", [P, PACK, V], F32)
         for t in range(PACK):
             nc.vector.tensor_copy(sum1[:, t, :], h[t][:].indirect(lists[0][:]))
-            nc.vector.tensor_copy(g_raw[:, t, :], h[t][:].indirect(half_of(cen_sb, 0, HV)))
+            if t < 2:
+                nc.vector.tensor_copy(g_raw[:, t, :], h[t][:].indirect(cen_sb[:]))
+            else:
+                nc.vector.tensor_copy(g_raw[:, t, 0:HV], h[t][:].indirect(half_of(cen_sb, 0, HV)))
         sum2 = sbuf("sum2", [P, PACK, V], F32, tag="x_codes")
         for t in range(PACK):
             nc.vector.tensor_tensor(sum2[:, t, :], h[t][:].indirect(lists[1][:]), sum1[:, t, :], ADD)
@@ -169,8 +172,10 @@ def tile_picked_sagecat_mean_lo_kernel(
 
         sum4 = last_sums("sum4_0", 0, None)
         zg_bf = sbuf("zg_bf", [P, 2, HV, PACK], BF16, tag="w_raw1")
-        nc.scalar.copy(woven(zg_bf[:, 1]), planes(g_raw[:]))
-        nc.scalar.activation(woven(zg_bf[:, 0]), planes(sum4[:]), COPY, scale=0.25)
+        nc.scalar.copy(woven(zg_bf[:, 1]), planes(g_raw[:, :, 0:HV]))
+        quarter = sbuf("quarter", [P, 1], F32)
+        nc.vector.memset(quarter[:], 0.25)
+        nc.scalar.activation(woven(zg_bf[:, 0]), planes(sum4[:]), COPY, scale=quarter[:])
         zg_codes = sbuf("zg_codes", [P, V], U32)
         zg_scales = sbuf("zg_scales", [P, V], U8)
         quantize(zg_codes[:], zg_scales[:], zg_bf[:].rearrange("p n c t -> p (n c) t"))
@@ -180,34 +185,29 @@ def tile_picked_sagecat_mean_lo_kernel(
                 cols = slice(number * HV, (number + 1) * HV)
                 second(whole[:, t, :], number, t, zg_codes[:, cols], zg_scales[:, cols])
 
-        y = sbuf("y0", [P, PACK, HV], F32)
-        nc.scalar.copy(y[:, 0:2, :], whole[:, 0:2, :])
-
-        sum4 = sbuf("sum4_1", [P, PACK, HV], F32, tag="sum4_0")
+        last = sbuf("last", [P, 6 * HV], F32, tag="sum4_0")
+        sum4 = last[:, 0 : 4 * HV].rearrange("p (t v) -> p t v", t=PACK)
+        g_bf = last[:, 4 * HV : 6 * HV].bitcast(BF16).rearrange("p (v t) -> p v t", t=PACK)
+        nc.scalar.copy(g_bf[:, :, 0:2], g_raw[:, 0:2, HV:V].rearrange("p t v -> p v t"))
         for t in range(PACK):
             earlier = sum3[t // 2][:, t % 2, HV:V]
             nc.vector.tensor_tensor(sum4[:, t, :], h[t][:].indirect(half_of(lists[3], 1, HV)), earlier, ADD)
-        z_bf = sbuf("z_bf", [P, HV, PACK], BF16, tag="zg_scales")
-        nc.scalar.activation(woven(z_bf[:]), planes(sum4[:]), COPY, scale=0.25)
+        z_bf = sbuf("z_bf", [P, HV, PACK], BF16)
+        nc.scalar.activation(woven(z_bf[:]), planes(sum4), COPY, scale=quarter[:])
+        for t in range(2, PACK):
+            nc.vector.tensor_copy(g_bf[:, :, t], h[t][:].indirect(half_of(cen_sb, 1, HV)))
         z_codes = sbuf("z_codes", [P, HV], U32)
         z_scales = sbuf("z_scales", [P, HV], U8)
         quantize(z_codes[:], z_scales[:], z_bf[:])
-        g_last = sbuf("g_last", [P, 4 * HV], F32, tag="sum3_0")
-        g_pair = g_last[:, 0 : 2 * HV].rearrange("p (t v) -> p t v", t=2)
-        g_bf = g_last[:, 2 * HV : 4 * HV].bitcast(BF16).rearrange("p (v t) -> p v t", t=PACK)
-        for t in range(2):
-            nc.vector.tensor_copy(g_pair[:, t, :], h[t][:].indirect(half_of(cen_sb, 1, HV)))
-        nc.scalar.copy(g_bf[:, :, 0:2], g_pair.rearrange("p t v -> p v t"))
-        for t in range(2, PACK):
-            nc.vector.tensor_copy(g_bf[:, :, t], h[t][:].indirect(half_of(cen_sb, 1, HV)))
         g_codes = sbuf("g_codes", [P, HV], U32)
-        g_scales = sbuf("g_scales", [P, HV], U8)
+        g_scales = sbuf("g_scales", [P, HV], U8, tag="quarter")
         quantize(g_codes[:], g_scales[:], g_bf)
 
-        nc.scalar.copy(y[:, 2:4, :], whole[:, 2:4, :])
+        y = sbuf("y0", [P, PACK, HV], F32)
+        nc.scalar.copy(y[:], whole[:])
         nc.sync.dma_start(out_rows[:, :, 0:HV], y[:])
         y_bf = sbuf("y_bf0", [P, HV, PACK], BF16)
-        nc.scalar.copy(woven(y_bf[:]), planes(whole[:]))
+        nc.vector.tensor_copy(woven(y_bf[:]), planes(y[:]))
         hand_out(0, y_bf)
 
         y = sbuf("y1", [P, PACK, HV], F32)

@@ -86,29 +86,38 @@ def tile_picked_sagecat_mean_lo_kernel(
         x_codes = sbuf("x_codes", [P, S], U32)
         x_scales = sbuf("x_scales", [P, S], U8)
         x_bf = [sbuf("x_bf%d" % a, [P, HS, PACK], BF16) for a in range(2)]
-        x_found = sbuf("x_found", [P, PACK, S], F32)
-        for j in range(PACK - 1):
+        x_found = sbuf("x_found", [P, PACK, S], BF16)
+        x0_bf = sbuf("x0_bf", [P, T], BF16)
+        nc.scalar.copy(x0_bf[:], x_raw[0][:])
+        nc.scalar.activation(x_found[:, 0, :], x0_bf[:].indirect(offs_sb[:]), COPY)
+        for j in range(1, PACK - 1):
             nc.vector.tensor_copy(x_found[:, j, :], x_raw[j][:].indirect(offs_sb[:]))
         for q in range(4):
             cols = slice(q * P, (q + 1) * P)
             nc.vector.tensor_copy(x_found[:, 3, cols], x_raw[3][:].indirect(offs_sb[:, q * P // 16 : (q + 1) * P // 16]))
-            weave = nc.scalar.copy if q < 2 else nc.vector.tensor_copy
-            weave(woven(x_bf[q // 2][:, (q % 2) * P : (q % 2 + 1) * P, :]), planes(x_found[:, :, cols]))
-        for a in range(2):
-            cols = slice(a * HS, (a + 1) * HS)
-            quantize(x_codes[:, cols], x_scales[:, cols], x_bf[a][:])
+            if q % 2 == 0:
+                nc.scalar.copy(woven(x_bf[q // 2][:, 0:P, :]), planes(x_found[:, :, cols]))
+        for q in (1, 3):
+            nc.vector.tensor_copy(woven(x_bf[q // 2][:, P:HS, :]), planes(x_found[:, :, q * P : (q + 1) * P]))
 
         w1_dealt = w1_raw[:].rearrange("p j (u t b) -> p t u j b", t=PACK, b=4)
         h = [sbuf("h%d" % t, [P, S], F32) for t in range(PACK)]
+
         w1_bf = []
-        for t in range(2):
-            rounded = sbuf("w1_bf%d" % t, [P, P, PACK], BF16)
-            nc.scalar.copy(rounded[:].rearrange("p (u b) j -> p u j b", b=4), w1_dealt[:, t])
+
+        def cast_w1(cast, t, rounded):
+            cast(rounded.rearrange("p (u b) j -> p u j b", b=4), w1_dealt[:, t])
             w1_bf.append(rounded)
+
+        for a in range(2):
+            cols = slice(a * HS, (a + 1) * HS)
+            quantize(x_codes[:, cols], x_scales[:, cols], x_bf[a][:])
+        for t in range(2):
+            cast_w1(nc.scalar.copy, t, sbuf("w1_bf%d" % t, [P, P, PACK], BF16)[:])
         for t in range(PACK):
             w1_codes = sbuf("w1_codes%d" % t, [P, P], U32)
             w1_scales = sbuf("w1_scales%d" % t, [P, P], U8)
-            quantize(w1_codes[:], w1_scales[:], w1_bf[t][:])
+            quantize(w1_codes[:], w1_scales[:], w1_bf[t])
             if t == 0:
                 for a in range(2):
                     cols = slice(a * HS, (a + 1) * HS)
@@ -118,14 +127,18 @@ def tile_picked_sagecat_mean_lo_kernel(
             else:
                 acc = bank(1 + t, "h_acc%d" % t, [P, S])
                 multiply(acc[:], w1_codes[:], w1_scales[:], x_codes[:], x_scales[:], True, True)
-                nc.scalar.activation(h[t][:], acc[:], RELU)
+                if t < 3:
+                    nc.scalar.activation(h[t][:], acc[:], RELU)
+                else:
+                    zero = sbuf("zero", [P, 1], F32)
+                    nc.vector.memset(zero[:], 0.0)
+                    nc.scalar.activation(h[t][:], acc[:], RELU, bias=zero[:])
+            if t == 0:
+                w1_late = sbuf("w1_late", [P, 2, P, PACK], BF16, tag="w1_bf0")
             if t < 2:
-                rounded = sbuf("w1_bf%d" % (t + 2), [P, P, PACK], BF16, tag=("w1_bf0", "w1_codes0")[t])
-                cast = (nc.vector.tensor_copy, nc.scalar.copy)[t]
-                cast(rounded[:].rearrange("p (u b) j -> p u j b", b=4), w1_dealt[:, t + 2])
-                w1_bf.append(rounded)
+                cast_w1(nc.vector.tensor_copy, t + 2, w1_late[:, t])
 
-        w_bf = sbuf("w_bf", [P, 2, H, PACK], BF16)
+        w_bf = sbuf("w_bf", [P, 2, H, PACK], BF16, tag="w1_codes3")
         for number in range(2):
             src = w_raw[number][:].rearrange("p j (m t) -> p m j t", t=PACK)
             dst = w_bf[:, number].rearrange("p (t m) j -> p m j t", t=PACK)
@@ -135,19 +148,20 @@ def tile_picked_sagecat_mean_lo_kernel(
         w_scales = sbuf("w_scales", [P, 2 * H], U8)
         quantize(w_codes[:], w_scales[:], w_bf[:].rearrange("p n c t -> p (n c) t"))
 
-        def second(acc, number, t, codes, scales):
+        def second(acc, number, t, codes, scales, opens=True, closes=True):
             m = slice(number * H + t * P, number * H + (t + 1) * P)
-            multiply(acc, w_codes[:, m], w_scales[:, m], codes, scales, number == 0, number == 1)
+            multiply(acc, w_codes[:, m], w_scales[:, m], codes, scales, number == 0 and opens, number == 1 and closes)
 
         sum1 = sbuf("sum1", [P, PACK, V], F32)
-        g_raw = sbuf("g_raw", [P, PACK, V], F32)
+        found = sbuf("found", [P, PACK + 1, V], F32)
+        g_raw = found[:, 0:PACK, :]
         for t in range(PACK):
             nc.vector.tensor_copy(sum1[:, t, :], h[t][:].indirect(lists[0][:]))
-            if t < 2:
+            if t < 1:
                 nc.vector.tensor_copy(g_raw[:, t, :], h[t][:].indirect(cen_sb[:]))
             else:
                 nc.vector.tensor_copy(g_raw[:, t, 0:HV], h[t][:].indirect(half_of(cen_sb, 0, HV)))
-        sum2 = sbuf("sum2", [P, PACK, V], F32, tag="x_codes")
+        sum2 = sbuf("sum2", [P, PACK, V], F32, tag="zero")
         for t in range(PACK):
             nc.vector.tensor_tensor(sum2[:, t, :], h[t][:].indirect(lists[1][:]), sum1[:, t, :], ADD)
         sum3 = [sbuf("sum3_%d" % u, [P, 2, V], F32) for u in range(2)]
@@ -159,23 +173,22 @@ def tile_picked_sagecat_mean_lo_kernel(
         out_rows = out_0.rearrange("(p t) v -> p t v", t=PACK)
         out_words = out_1[0].rearrange("p c r -> p (c r)").bitcast(I32)
 
-        def last_sums(name, a, tag):
-            sum4 = sbuf(name, [P, PACK, HV], F32, tag=tag)
+        def last_sums(sum4, a):
             for t in range(PACK):
                 earlier = sum3[t // 2][:, t % 2, a * HV : (a + 1) * HV]
                 nc.vector.tensor_tensor(sum4[:, t, :], h[t][:].indirect(half_of(lists[3], a, HV)), earlier, ADD)
-            return sum4
 
         def hand_out(a, y_bf):
             cols = slice(a * HV, (a + 1) * HV)
             quantize(y_codes[:, cols], y_scales[:, cols], y_bf[:])
 
-        sum4 = last_sums("sum4_0", 0, None)
+        sum4 = found[:, 1 : PACK + 1, HV:V]
+        last_sums(sum4, 0)
         zg_bf = sbuf("zg_bf", [P, 2, HV, PACK], BF16, tag="w_raw1")
         nc.scalar.copy(woven(zg_bf[:, 1]), planes(g_raw[:, :, 0:HV]))
         quarter = sbuf("quarter", [P, 1], F32)
         nc.vector.memset(quarter[:], 0.25)
-        nc.scalar.activation(woven(zg_bf[:, 0]), planes(sum4[:]), COPY, scale=quarter[:])
+        nc.scalar.activation(woven(zg_bf[:, 0]), planes(sum4), COPY, scale=quarter[:])
         zg_codes = sbuf("zg_codes", [P, V], U32)
         zg_scales = sbuf("zg_scales", [P, V], U8)
         quantize(zg_codes[:], zg_scales[:], zg_bf[:].rearrange("p n c t -> p (n c) t"))
@@ -185,22 +198,23 @@ def tile_picked_sagecat_mean_lo_kernel(
                 cols = slice(number * HV, (number + 1) * HV)
                 second(whole[:, t, :], number, t, zg_codes[:, cols], zg_scales[:, cols])
 
-        last = sbuf("last", [P, 6 * HV], F32, tag="sum4_0")
+        last = sbuf("last", [P, 6 * HV], F32, tag="quarter")
         sum4 = last[:, 0 : 4 * HV].rearrange("p (t v) -> p t v", t=PACK)
         g_bf = last[:, 4 * HV : 6 * HV].bitcast(BF16).rearrange("p (v t) -> p v t", t=PACK)
-        nc.scalar.copy(g_bf[:, :, 0:2], g_raw[:, 0:2, HV:V].rearrange("p t v -> p v t"))
-        for t in range(PACK):
-            earlier = sum3[t // 2][:, t % 2, HV:V]
-            nc.vector.tensor_tensor(sum4[:, t, :], h[t][:].indirect(half_of(lists[3], 1, HV)), earlier, ADD)
+        last_sums(sum4, 1)
         z_bf = sbuf("z_bf", [P, HV, PACK], BF16)
+        quarter = sbuf("quarter1", [P, 1], F32)
+        nc.vector.memset(quarter[:], 0.25)
         nc.scalar.activation(woven(z_bf[:]), planes(sum4), COPY, scale=quarter[:])
+        nc.vector.tensor_copy(g_raw[:, 1, HV:V], h[1][:].indirect(half_of(cen_sb, 1, HV)))
+        nc.scalar.copy(g_bf[:, :, 0:2], g_raw[:, 0:2, HV:V].rearrange("p t v -> p v t"))
         for t in range(2, PACK):
             nc.vector.tensor_copy(g_bf[:, :, t], h[t][:].indirect(half_of(cen_sb, 1, HV)))
         z_codes = sbuf("z_codes", [P, HV], U32)
         z_scales = sbuf("z_scales", [P, HV], U8)
         quantize(z_codes[:], z_scales[:], z_bf[:])
         g_codes = sbuf("g_codes", [P, HV], U32)
-        g_scales = sbuf("g_scales", [P, HV], U8, tag="quarter")
+        g_scales = sbuf("g_scales", [P, HV], U8, tag="quarter1")
         quantize(g_codes[:], g_scales[:], g_bf)
 
         y = sbuf("y0", [P, PACK, HV], F32)
@@ -214,12 +228,10 @@ def tile_picked_sagecat_mean_lo_kernel(
         y_bf = sbuf("y_bf1", [P, HV, PACK], BF16)
         last_pair = bank(6, "y_acc_pair", [P, 2, HV])
         accs = [bank(7, "y_acc0", [P, HV])[:], bank(0, "y_acc1", [P, HV])[:], last_pair[:, 0, :], last_pair[:, 1, :]]
-        for t in range(3):
-            second(accs[t], 0, t, z_codes[:], z_scales[:])
-        for t in range(3):
-            second(accs[t], 1, t, g_codes[:], g_scales[:])
-        second(accs[3], 0, 3, z_codes[:], z_scales[:])
-        second(accs[3], 1, 3, g_codes[:], g_scales[:])
+        for t in range(PACK):
+            second(accs[t], 0, t, z_codes[:], z_scales[:], opens=t != 3)
+        for t in range(PACK):
+            second(accs[t], 1, t, g_codes[:], g_scales[:], closes=t != 2)
         for t in range(2):
             nc.scalar.copy(y[:, t, :], accs[t])
         nc.sync.dma_start(out_rows[:, 0:2, HV:V], y[:, 0:2, :])

@@ -86,59 +86,48 @@ def tile_picked_sagecat_mean_lo_kernel(
         x_codes = sbuf("x_codes", [P, S], U32)
         x_scales = sbuf("x_scales", [P, S], U8)
         x_bf = [sbuf("x_bf%d" % a, [P, HS, PACK], BF16) for a in range(2)]
-        x_found = sbuf("x_found", [P, PACK, S], BF16)
-        x0_bf = sbuf("x0_bf", [P, T], BF16)
-        nc.scalar.copy(x0_bf[:], x_raw[0][:])
-        nc.scalar.activation(x_found[:, 0, :], x0_bf[:].indirect(offs_sb[:]), COPY)
-        for j in range(1, PACK - 1):
+        x_found = sbuf("x_found", [P, PACK, S], F32)
+        for j in range(PACK - 1):
             nc.vector.tensor_copy(x_found[:, j, :], x_raw[j][:].indirect(offs_sb[:]))
         for q in range(4):
             cols = slice(q * P, (q + 1) * P)
             nc.vector.tensor_copy(x_found[:, 3, cols], x_raw[3][:].indirect(offs_sb[:, q * P // 16 : (q + 1) * P // 16]))
-            if q % 2 == 0:
-                nc.scalar.copy(woven(x_bf[q // 2][:, 0:P, :]), planes(x_found[:, :, cols]))
-        for q in (1, 3):
-            nc.vector.tensor_copy(woven(x_bf[q // 2][:, P:HS, :]), planes(x_found[:, :, q * P : (q + 1) * P]))
-
-        w1_dealt = w1_raw[:].rearrange("p j (u t b) -> p t u j b", t=PACK, b=4)
-        h = [sbuf("h%d" % t, [P, S], F32) for t in range(PACK)]
-
-        w1_bf = []
-
-        def cast_w1(cast, t, rounded):
-            cast(rounded.rearrange("p (u b) j -> p u j b", b=4), w1_dealt[:, t])
-            w1_bf.append(rounded)
-
+            weave = nc.scalar.copy if q % 2 == 0 else nc.vector.tensor_copy
+            weave(woven(x_bf[q // 2][:, (q % 2) * P : (q % 2 + 1) * P, :]), planes(x_found[:, :, cols]))
         for a in range(2):
             cols = slice(a * HS, (a + 1) * HS)
             quantize(x_codes[:, cols], x_scales[:, cols], x_bf[a][:])
+
+        w1_dealt = w1_raw[:].rearrange("p j (u t b) -> p t u j b", t=PACK, b=4)
+        h = [sbuf("h%d" % t, [P, S], F32) for t in range(PACK)]
+        w1_bf = []
+
+        def round_w1(t, cast, tag):
+            rounded = sbuf("w1_bf%d" % t, [P, P, PACK], BF16, tag=tag)
+            cast(rounded[:].rearrange("p (u b) j -> p u j b", b=4), w1_dealt[:, t])
+            w1_bf.append(rounded)
+
         for t in range(2):
-            cast_w1(nc.scalar.copy, t, sbuf("w1_bf%d" % t, [P, P, PACK], BF16)[:])
+            round_w1(t, nc.scalar.copy, None)
         for t in range(PACK):
             w1_codes = sbuf("w1_codes%d" % t, [P, P], U32)
             w1_scales = sbuf("w1_scales%d" % t, [P, P], U8)
-            quantize(w1_codes[:], w1_scales[:], w1_bf[t])
+            quantize(w1_codes[:], w1_scales[:], w1_bf[t][:])
             if t == 0:
                 for a in range(2):
                     cols = slice(a * HS, (a + 1) * HS)
                     acc = bank(a, "h0_acc%d" % a, [P, HS])
                     multiply(acc[:], w1_codes[:], w1_scales[:], x_codes[:, cols], x_scales[:, cols], True, True)
                     nc.scalar.activation(h[0][:, cols], acc[:], RELU)
+                round_w1(2, nc.vector.tensor_copy, "w1_bf0")
             else:
                 acc = bank(1 + t, "h_acc%d" % t, [P, S])
                 multiply(acc[:], w1_codes[:], w1_scales[:], x_codes[:], x_scales[:], True, True)
-                if t < 3:
-                    nc.scalar.activation(h[t][:], acc[:], RELU)
-                else:
-                    zero = sbuf("zero", [P, 1], F32)
-                    nc.vector.memset(zero[:], 0.0)
-                    nc.scalar.activation(h[t][:], acc[:], RELU, bias=zero[:])
-            if t == 0:
-                w1_late = sbuf("w1_late", [P, 2, P, PACK], BF16, tag="w1_bf0")
-            if t < 2:
-                cast_w1(nc.vector.tensor_copy, t + 2, w1_late[:, t])
+                nc.scalar.activation(h[t][:], acc[:], RELU)
+            if t == 1:
+                round_w1(3, nc.scalar.copy, "w1_codes0")
 
-        w_bf = sbuf("w_bf", [P, 2, H, PACK], BF16, tag="w1_codes3")
+        w_bf = sbuf("w_bf", [P, 2, H, PACK], BF16)
         for number in range(2):
             src = w_raw[number][:].rearrange("p j (m t) -> p m j t", t=PACK)
             dst = w_bf[:, number].rearrange("p (t m) j -> p m j t", t=PACK)
@@ -148,20 +137,20 @@ def tile_picked_sagecat_mean_lo_kernel(
         w_scales = sbuf("w_scales", [P, 2 * H], U8)
         quantize(w_codes[:], w_scales[:], w_bf[:].rearrange("p n c t -> p (n c) t"))
 
-        def second(acc, number, t, codes, scales, opens=True, closes=True):
+        def second(acc, number, t, codes, scales, start, stop):
             m = slice(number * H + t * P, number * H + (t + 1) * P)
-            multiply(acc, w_codes[:, m], w_scales[:, m], codes, scales, number == 0 and opens, number == 1 and closes)
+            multiply(acc, w_codes[:, m], w_scales[:, m], codes, scales, start, stop)
 
         sum1 = sbuf("sum1", [P, PACK, V], F32)
         found = sbuf("found", [P, PACK + 1, V], F32)
         g_raw = found[:, 0:PACK, :]
         for t in range(PACK):
             nc.vector.tensor_copy(sum1[:, t, :], h[t][:].indirect(lists[0][:]))
-            if t < 1:
+            if t == 0:
                 nc.vector.tensor_copy(g_raw[:, t, :], h[t][:].indirect(cen_sb[:]))
             else:
                 nc.vector.tensor_copy(g_raw[:, t, 0:HV], h[t][:].indirect(half_of(cen_sb, 0, HV)))
-        sum2 = sbuf("sum2", [P, PACK, V], F32, tag="zero")
+        sum2 = sbuf("sum2", [P, PACK, V], F32, tag="x_codes")
         for t in range(PACK):
             nc.vector.tensor_tensor(sum2[:, t, :], h[t][:].indirect(lists[1][:]), sum1[:, t, :], ADD)
         sum3 = [sbuf("sum3_%d" % u, [P, 2, V], F32) for u in range(2)]
@@ -182,13 +171,13 @@ def tile_picked_sagecat_mean_lo_kernel(
             cols = slice(a * HV, (a + 1) * HV)
             quantize(y_codes[:, cols], y_scales[:, cols], y_bf[:])
 
-        sum4 = found[:, 1 : PACK + 1, HV:V]
-        last_sums(sum4, 0)
+        first_sums = found[:, 1 : PACK + 1, HV:V]
+        last_sums(first_sums, 0)
         zg_bf = sbuf("zg_bf", [P, 2, HV, PACK], BF16, tag="w_raw1")
         nc.scalar.copy(woven(zg_bf[:, 1]), planes(g_raw[:, :, 0:HV]))
-        quarter = sbuf("quarter", [P, 1], F32)
-        nc.vector.memset(quarter[:], 0.25)
-        nc.scalar.activation(woven(zg_bf[:, 0]), planes(sum4), COPY, scale=quarter[:])
+        first_quarter = sbuf("first_quarter", [P, 1], F32)
+        nc.vector.memset(first_quarter[:], 0.25)
+        nc.scalar.activation(woven(zg_bf[:, 0]), planes(first_sums), COPY, scale=first_quarter[:])
         zg_codes = sbuf("zg_codes", [P, V], U32)
         zg_scales = sbuf("zg_scales", [P, V], U8)
         quantize(zg_codes[:], zg_scales[:], zg_bf[:].rearrange("p n c t -> p (n c) t"))
@@ -196,16 +185,16 @@ def tile_picked_sagecat_mean_lo_kernel(
         for t in range(PACK):
             for number in range(2):
                 cols = slice(number * HV, (number + 1) * HV)
-                second(whole[:, t, :], number, t, zg_codes[:, cols], zg_scales[:, cols])
+                second(whole[:, t, :], number, t, zg_codes[:, cols], zg_scales[:, cols], number == 0, number == 1)
 
-        last = sbuf("last", [P, 6 * HV], F32, tag="quarter")
-        sum4 = last[:, 0 : 4 * HV].rearrange("p (t v) -> p t v", t=PACK)
+        last = sbuf("last", [P, 6 * HV], F32, tag="first_quarter")
+        second_sums = last[:, 0 : 4 * HV].rearrange("p (t v) -> p t v", t=PACK)
         g_bf = last[:, 4 * HV : 6 * HV].bitcast(BF16).rearrange("p (v t) -> p v t", t=PACK)
-        last_sums(sum4, 1)
+        last_sums(second_sums, 1)
         z_bf = sbuf("z_bf", [P, HV, PACK], BF16)
-        quarter = sbuf("quarter1", [P, 1], F32)
-        nc.vector.memset(quarter[:], 0.25)
-        nc.scalar.activation(woven(z_bf[:]), planes(sum4), COPY, scale=quarter[:])
+        second_quarter = sbuf("second_quarter", [P, 1], F32)
+        nc.vector.memset(second_quarter[:], 0.25)
+        nc.scalar.activation(woven(z_bf[:]), planes(second_sums), COPY, scale=second_quarter[:])
         nc.vector.tensor_copy(g_raw[:, 1, HV:V], h[1][:].indirect(half_of(cen_sb, 1, HV)))
         nc.scalar.copy(g_bf[:, :, 0:2], g_raw[:, 0:2, HV:V].rearrange("p t v -> p v t"))
         for t in range(2, PACK):
@@ -214,32 +203,33 @@ def tile_picked_sagecat_mean_lo_kernel(
         z_scales = sbuf("z_scales", [P, HV], U8)
         quantize(z_codes[:], z_scales[:], z_bf[:])
         g_codes = sbuf("g_codes", [P, HV], U32)
-        g_scales = sbuf("g_scales", [P, HV], U8, tag="quarter1")
+        g_scales = sbuf("g_scales", [P, HV], U8, tag="second_quarter")
         quantize(g_codes[:], g_scales[:], g_bf)
 
-        y = sbuf("y0", [P, PACK, HV], F32)
-        nc.scalar.copy(y[:], whole[:])
-        nc.sync.dma_start(out_rows[:, :, 0:HV], y[:])
-        y_bf = sbuf("y_bf0", [P, HV, PACK], BF16)
-        nc.vector.tensor_copy(woven(y_bf[:]), planes(y[:]))
-        hand_out(0, y_bf)
+        y_first = sbuf("y_first", [P, PACK, HV], F32)
+        nc.scalar.copy(y_first[:], whole[:])
+        nc.sync.dma_start(out_rows[:, :, 0:HV], y_first[:])
+        y_first_bf = sbuf("y_first_bf", [P, HV, PACK], BF16)
+        nc.vector.tensor_copy(woven(y_first_bf[:]), planes(y_first[:]))
+        hand_out(0, y_first_bf)
 
-        y = sbuf("y1", [P, PACK, HV], F32)
-        y_bf = sbuf("y_bf1", [P, HV, PACK], BF16)
+        y_second = sbuf("y_second", [P, PACK, HV], F32)
+        y_second_bf = sbuf("y_second_bf", [P, HV, PACK], BF16)
         last_pair = bank(6, "y_acc_pair", [P, 2, HV])
         accs = [bank(7, "y_acc0", [P, HV])[:], bank(0, "y_acc1", [P, HV])[:], last_pair[:, 0, :], last_pair[:, 1, :]]
         for t in range(PACK):
-            second(accs[t], 0, t, z_codes[:], z_scales[:], opens=t != 3)
+            second(accs[t], 0, t, z_codes[:], z_scales[:], t != 3, False)
         for t in range(PACK):
-            second(accs[t], 1, t, g_codes[:], g_scales[:], closes=t != 2)
+            second(accs[t], 1, t, g_codes[:], g_scales[:], False, t != 2)
         for t in range(2):
-            nc.scalar.copy(y[:, t, :], accs[t])
-        nc.sync.dma_start(out_rows[:, 0:2, HV:V], y[:, 0:2, :])
-        nc.vector.tensor_copy(y_bf[:, :, 0:2], y[:, 0:2, :].rearrange("p t v -> p v t"))
-        nc.scalar.copy(y_bf[:, :, 2:4], last_pair[:].rearrange("p t v -> p v t"))
-        nc.scalar.copy(y[:, 2:4, :], last_pair[:])
-        nc.scalar.dma_start(out_rows[:, 2:4, HV:V], y[:, 2:4, :])
-        hand_out(1, y_bf)
+            nc.scalar.copy(y_second[:, t, :], accs[t])
+        nc.sync.dma_start(out_rows[:, 0:2, HV:V], y_second[:, 0:2, :])
+        nc.vector.tensor_copy(y_second_bf[:, :, 0:2], y_second[:, 0:2, :].rearrange("p t v -> p v t"))
+        nc.scalar.copy(y_second_bf[:, :, 2:4], last_pair[:].rearrange("p t v -> p v t"))
+        nc.scalar.copy(y_second[:, 2:4, :], last_pair[:])
+        nc.scalar.dma_start(out_rows[:, 2:4, HV:V], y_second[:, 2:4, :])
+        hand_out(1, y_second_bf)
+
         nc.sync.dma_start(out_words, y_codes[:].bitcast(I32))
         for q in range(4):
             queue = nc.scalar if q >= 2 else nc.sync

@@ -118,16 +118,23 @@ def tile_picked_sagecat_mean_lo_kernel(
                     cols = slice(a * HS, (a + 1) * HS)
                     acc = bank(a, "h0_acc%d" % a, [P, HS])
                     multiply(acc[:], w1_codes[:], w1_scales[:], x_codes[:, cols], x_scales[:, cols], True, True)
-                    nc.scalar.activation(h[0][:, cols], acc[:], RELU)
+                    if a == 0:
+                        nc.vector.tensor_scalar_max(h[0][:, cols], acc[:], 0.0)
+                    else:
+                        nc.scalar.activation(h[0][:, cols], acc[:], RELU)
                 round_w1(2, nc.vector.tensor_copy, "w1_bf0")
+                round_w1(3, nc.scalar.copy, None)
             else:
                 acc = bank(1 + t, "h_acc%d" % t, [P, S])
                 multiply(acc[:], w1_codes[:], w1_scales[:], x_codes[:], x_scales[:], True, True)
-                nc.scalar.activation(h[t][:], acc[:], RELU)
-            if t == 1:
-                round_w1(3, nc.scalar.copy, "w1_codes0")
+                if t < 3:
+                    nc.scalar.activation(h[t][:], acc[:], RELU)
+                else:
+                    zero = sbuf("zero", [P, 1], F32)
+                    nc.vector.memset(zero[:], 0.0)
+                    nc.scalar.activation(h[t][:], acc[:], RELU, bias=zero[:])
 
-        w_bf = sbuf("w_bf", [P, 2, H, PACK], BF16)
+        w_bf = sbuf("w_bf", [P, 2, H, PACK], BF16, tag="w1_codes3")
         for number in range(2):
             src = w_raw[number][:].rearrange("p j (m t) -> p m j t", t=PACK)
             dst = w_bf[:, number].rearrange("p (t m) j -> p m j t", t=PACK)
@@ -150,7 +157,7 @@ def tile_picked_sagecat_mean_lo_kernel(
                 nc.vector.tensor_copy(g_raw[:, t, :], h[t][:].indirect(cen_sb[:]))
             else:
                 nc.vector.tensor_copy(g_raw[:, t, 0:HV], h[t][:].indirect(half_of(cen_sb, 0, HV)))
-        sum2 = sbuf("sum2", [P, PACK, V], F32, tag="x_codes")
+        sum2 = sbuf("sum2", [P, PACK, V], F32, tag="zero")
         for t in range(PACK):
             nc.vector.tensor_tensor(sum2[:, t, :], h[t][:].indirect(lists[1][:]), sum1[:, t, :], ADD)
         sum3 = [sbuf("sum3_%d" % u, [P, 2, V], F32) for u in range(2)]

@@ -13,6 +13,8 @@ U16 = mybir.dt.uint16
 U8 = mybir.dt.uint8
 FP8X4 = mybir.dt.float8_e4m3fn_x4
 ADD = mybir.AluOpType.add
+MAX = mybir.AluOpType.max
+MULT = mybir.AluOpType.mult
 COPY = mybir.ActivationFunctionType.Copy
 RELU = mybir.ActivationFunctionType.Relu
 
@@ -83,17 +85,20 @@ def tile_picked_sagecat_mean_lo_kernel(
         def half_of(list_sb, half, entries):
             return list_sb[:, half * entries // 16 : (half + 1) * entries // 16]
 
+        def fetch(out, window, offsets, factor=1.0):
+            nc.scalar.activation(out, window.indirect(offsets), COPY, scale=factor)
+
         x_codes = sbuf("x_codes", [P, S], U32)
         x_scales = sbuf("x_scales", [P, S], U8)
         x_bf = [sbuf("x_bf%d" % a, [P, HS, PACK], BF16) for a in range(2)]
-        x_found = sbuf("x_found", [P, PACK, S], F32)
-        for j in range(PACK - 1):
-            nc.vector.tensor_copy(x_found[:, j, :], x_raw[j][:].indirect(offs_sb[:]))
-        for q in range(4):
-            cols = slice(q * P, (q + 1) * P)
-            nc.vector.tensor_copy(x_found[:, 3, cols], x_raw[3][:].indirect(offs_sb[:, q * P // 16 : (q + 1) * P // 16]))
-            weave = nc.scalar.copy if q % 2 == 0 else nc.vector.tensor_copy
-            weave(woven(x_bf[q // 2][:, (q % 2) * P : (q % 2 + 1) * P, :]), planes(x_found[:, :, cols]))
+        x_found = [sbuf("x_found%d" % a, [P, PACK, HS], F32) for a in range(2)]
+        for j in range(PACK):
+            nc.vector.tensor_copy(x_found[0][:, j, :], x_raw[j][:].indirect(half_of(offs_sb, 0, HS)))
+            fetch(x_found[1][:, j, :], x_raw[j][:], half_of(offs_sb, 1, HS))
+        nc.scalar.copy(woven(x_bf[1][:, 0:P, :]), planes(x_found[1][:, :, 0:P]))
+        for q in range(2):
+            nc.vector.tensor_copy(woven(x_bf[0][:, q * P : (q + 1) * P, :]), planes(x_found[0][:, :, q * P : (q + 1) * P]))
+        nc.vector.tensor_copy(woven(x_bf[1][:, P:HS, :]), planes(x_found[1][:, :, P:HS]))
         for a in range(2):
             cols = slice(a * HS, (a + 1) * HS)
             quantize(x_codes[:, cols], x_scales[:, cols], x_bf[a][:])
@@ -101,14 +106,11 @@ def tile_picked_sagecat_mean_lo_kernel(
         w1_dealt = w1_raw[:].rearrange("p j (u t b) -> p t u j b", t=PACK, b=4)
         h = [sbuf("h%d" % t, [P, S], F32) for t in range(PACK)]
         w1_bf = []
-
-        def round_w1(t, cast, tag):
-            rounded = sbuf("w1_bf%d" % t, [P, P, PACK], BF16, tag=tag)
+        for t in range(PACK):
+            rounded = sbuf("w1_bf%d" % t, [P, P, PACK], BF16)
+            cast = nc.scalar.copy if t in (0, 3) else nc.vector.tensor_copy
             cast(rounded[:].rearrange("p (u b) j -> p u j b", b=4), w1_dealt[:, t])
             w1_bf.append(rounded)
-
-        for t in range(2):
-            round_w1(t, nc.scalar.copy, None)
         for t in range(PACK):
             w1_codes = sbuf("w1_codes%d" % t, [P, P], U32)
             w1_scales = sbuf("w1_scales%d" % t, [P, P], U8)
@@ -119,72 +121,69 @@ def tile_picked_sagecat_mean_lo_kernel(
                     acc = bank(a, "h0_acc%d" % a, [P, HS])
                     multiply(acc[:], w1_codes[:], w1_scales[:], x_codes[:, cols], x_scales[:, cols], True, True)
                     if a == 0:
-                        nc.vector.tensor_scalar_max(h[0][:, cols], acc[:], 0.0)
+                        nc.vector.tensor_scalar(h[0][:, cols], acc[:], 0.0, 0.25, MAX, MULT)
                     else:
-                        nc.scalar.activation(h[0][:, cols], acc[:], RELU)
-                round_w1(2, nc.vector.tensor_copy, "w1_bf0")
-                round_w1(3, nc.scalar.copy, None)
+                        nc.scalar.activation(h[0][:, cols], acc[:], RELU, scale=0.25)
             else:
                 acc = bank(1 + t, "h_acc%d" % t, [P, S])
                 multiply(acc[:], w1_codes[:], w1_scales[:], x_codes[:], x_scales[:], True, True)
-                if t < 3:
-                    nc.scalar.activation(h[t][:], acc[:], RELU)
-                else:
-                    zero = sbuf("zero", [P, 1], F32)
-                    nc.vector.memset(zero[:], 0.0)
-                    nc.scalar.activation(h[t][:], acc[:], RELU, bias=zero[:])
+                nc.scalar.activation(h[t][:], acc[:], RELU, scale=0.25)
 
-        w_bf = sbuf("w_bf", [P, 2, H, PACK], BF16, tag="w1_codes3")
-        for number in range(2):
-            src = w_raw[number][:].rearrange("p j (m t) -> p m j t", t=PACK)
-            dst = w_bf[:, number].rearrange("p (t m) j -> p m j t", t=PACK)
-            for q in range(4):
-                nc.scalar.copy(dst[:, 32 * q : 32 * (q + 1)], src[:, 32 * q : 32 * (q + 1)])
         w_codes = sbuf("w_codes", [P, 2 * H], U32)
         w_scales = sbuf("w_scales", [P, 2 * H], U8)
-        quantize(w_codes[:], w_scales[:], w_bf[:].rearrange("p n c t -> p (n c) t"))
+
+        def second_weights(number):
+            w_bf = [sbuf("w_bf%d_%d" % (number, e), [P, H // 2, PACK], BF16) for e in range(2)]
+            src = w_raw[number][:].rearrange("p j (m e t) -> p e m j t", e=2, t=2)
+            for e in range(2):
+                nc.vector.tensor_copy(w_bf[e][:].rearrange("p (t m) j -> p m j t", t=2), src[:, e])
+            for e in range(2):
+                cols = slice(number * H + e * H // 2, number * H + (e + 1) * H // 2)
+                quantize(w_codes[:, cols], w_scales[:, cols], w_bf[e][:])
 
         def second(acc, number, t, codes, scales, start, stop):
             m = slice(number * H + t * P, number * H + (t + 1) * P)
             multiply(acc, w_codes[:, m], w_scales[:, m], codes, scales, start, stop)
 
-        sum1 = sbuf("sum1", [P, PACK, V], F32)
-        found = sbuf("found", [P, PACK + 1, V], F32)
-        g_raw = found[:, 0:PACK, :]
-        for t in range(PACK):
-            nc.vector.tensor_copy(sum1[:, t, :], h[t][:].indirect(lists[0][:]))
-            if t == 0:
-                nc.vector.tensor_copy(g_raw[:, t, :], h[t][:].indirect(cen_sb[:]))
-            else:
-                nc.vector.tensor_copy(g_raw[:, t, 0:HV], h[t][:].indirect(half_of(cen_sb, 0, HV)))
-        sum2 = sbuf("sum2", [P, PACK, V], F32, tag="zero")
-        for t in range(PACK):
-            nc.vector.tensor_tensor(sum2[:, t, :], h[t][:].indirect(lists[1][:]), sum1[:, t, :], ADD)
-        sum3 = [sbuf("sum3_%d" % u, [P, 2, V], F32) for u in range(2)]
-        for t in range(PACK):
-            nc.vector.tensor_tensor(sum3[t // 2][:, t % 2, :], h[t][:].indirect(lists[2][:]), sum2[:, t, :], ADD)
+        def fetch_all(name, list_sb, a, factor=1.0, tag=None):
+            found = sbuf(name, [P, PACK, HV], F32, tag=tag)
+            for t in range(PACK):
+                fetch(found[:, t, :], h[t][:], half_of(list_sb, a, HV), factor)
+            return found
+
+        def add_all(name, list_sb, a, earlier, tag=None):
+            total = sbuf(name, [P, PACK, HV], F32, tag=tag)
+            for t in range(PACK):
+                nc.vector.tensor_tensor(total[:, t, :], h[t][:].indirect(half_of(list_sb, a, HV)), earlier[:, t, :], ADD)
+            return total
+
+        def join(z_bf, left, right):
+            nc.vector.tensor_tensor(
+                z_bf.rearrange("p (c i) t -> p c t i", i=2),
+                left.rearrange("p t (c i) -> p c t i", i=2),
+                right.rearrange("p t (c i) -> p c t i", i=2),
+                ADD,
+            )
 
         y_codes = sbuf("y_codes", [P, V], U32)
         y_scales = sbuf("y_scales", [P, V], U8)
         out_rows = out_0.rearrange("(p t) v -> p t v", t=PACK)
         out_words = out_1[0].rearrange("p c r -> p (c r)").bitcast(I32)
 
-        def last_sums(sum4, a):
-            for t in range(PACK):
-                earlier = sum3[t // 2][:, t % 2, a * HV : (a + 1) * HV]
-                nc.vector.tensor_tensor(sum4[:, t, :], h[t][:].indirect(half_of(lists[3], a, HV)), earlier, ADD)
-
         def hand_out(a, y_bf):
             cols = slice(a * HV, (a + 1) * HV)
             quantize(y_codes[:, cols], y_scales[:, cols], y_bf[:])
 
-        first_sums = found[:, 1 : PACK + 1, HV:V]
-        last_sums(first_sums, 0)
-        zg_bf = sbuf("zg_bf", [P, 2, HV, PACK], BF16, tag="w_raw1")
-        nc.scalar.copy(woven(zg_bf[:, 1]), planes(g_raw[:, :, 0:HV]))
-        first_quarter = sbuf("first_quarter", [P, 1], F32)
-        nc.vector.memset(first_quarter[:], 0.25)
-        nc.scalar.activation(woven(zg_bf[:, 0]), planes(first_sums), COPY, scale=first_quarter[:])
+        second_weights(0)
+        one = fetch_all("one0", lists[0], 0)
+        two = add_all("two0", lists[1], 0, one, tag="w_raw0")
+        second_weights(1)
+        three = fetch_all("three0", lists[2], 0)
+        four = add_all("four0", lists[3], 0, three, tag="w_raw1")
+        centres = fetch_all("centres0", cen_sb, 0, 4.0)
+        zg_bf = sbuf("zg_bf", [P, 2, HV, PACK], BF16)
+        nc.scalar.copy(woven(zg_bf[:, 1]), planes(centres[:]))
+        join(zg_bf[:, 0], two[:], four[:])
         zg_codes = sbuf("zg_codes", [P, V], U32)
         zg_scales = sbuf("zg_scales", [P, V], U8)
         quantize(zg_codes[:], zg_scales[:], zg_bf[:].rearrange("p n c t -> p (n c) t"))
@@ -194,30 +193,27 @@ def tile_picked_sagecat_mean_lo_kernel(
                 cols = slice(number * HV, (number + 1) * HV)
                 second(whole[:, t, :], number, t, zg_codes[:, cols], zg_scales[:, cols], number == 0, number == 1)
 
-        last = sbuf("last", [P, 6 * HV], F32, tag="first_quarter")
-        second_sums = last[:, 0 : 4 * HV].rearrange("p (t v) -> p t v", t=PACK)
-        g_bf = last[:, 4 * HV : 6 * HV].bitcast(BF16).rearrange("p (v t) -> p v t", t=PACK)
-        last_sums(second_sums, 1)
+        one = fetch_all("one1", lists[0], 1, tag="w1_codes3")
+        two = add_all("two1", lists[1], 1, one, tag="three0")
+        three = fetch_all("three1", lists[2], 1, tag="w1_scales3")
+        four = add_all("four1", lists[3], 1, three, tag="w_raw0")
+        centres = fetch_all("centres1", cen_sb, 1, 4.0, tag="x_codes")
+        g_bf = sbuf("g_bf", [P, HV, PACK], BF16, tag="w1_codes3")
+        nc.vector.tensor_copy(woven(g_bf[:]), planes(centres[:]))
         z_bf = sbuf("z_bf", [P, HV, PACK], BF16)
-        second_quarter = sbuf("second_quarter", [P, 1], F32)
-        nc.vector.memset(second_quarter[:], 0.25)
-        nc.scalar.activation(woven(z_bf[:]), planes(second_sums), COPY, scale=second_quarter[:])
-        nc.vector.tensor_copy(g_raw[:, 1, HV:V], h[1][:].indirect(half_of(cen_sb, 1, HV)))
-        nc.scalar.copy(g_bf[:, :, 0:2], g_raw[:, 0:2, HV:V].rearrange("p t v -> p v t"))
-        for t in range(2, PACK):
-            nc.vector.tensor_copy(g_bf[:, :, t], h[t][:].indirect(half_of(cen_sb, 1, HV)))
+        join(z_bf[:], two[:], four[:])
+        g_codes = sbuf("g_codes", [P, HV], U32)
+        g_scales = sbuf("g_scales", [P, HV], U8)
+        quantize(g_codes[:], g_scales[:], g_bf[:])
         z_codes = sbuf("z_codes", [P, HV], U32)
         z_scales = sbuf("z_scales", [P, HV], U8)
         quantize(z_codes[:], z_scales[:], z_bf[:])
-        g_codes = sbuf("g_codes", [P, HV], U32)
-        g_scales = sbuf("g_scales", [P, HV], U8, tag="second_quarter")
-        quantize(g_codes[:], g_scales[:], g_bf)
 
         y_first = sbuf("y_first", [P, PACK, HV], F32)
         nc.scalar.copy(y_first[:], whole[:])
         nc.sync.dma_start(out_rows[:, :, 0:HV], y_first[:])
         y_first_bf = sbuf("y_first_bf", [P, HV, PACK], BF16)
-        nc.vector.tensor_copy(woven(y_first_bf[:]), planes(y_first[:]))
+        nc.scalar.copy(woven(y_first_bf[:]), planes(y_first[:]))
         hand_out(0, y_first_bf)
 
         y_second = sbuf("y_second", [P, PACK, HV], F32)
@@ -225,9 +221,9 @@ def tile_picked_sagecat_mean_lo_kernel(
         last_pair = bank(6, "y_acc_pair", [P, 2, HV])
         accs = [bank(7, "y_acc0", [P, HV])[:], bank(0, "y_acc1", [P, HV])[:], last_pair[:, 0, :], last_pair[:, 1, :]]
         for t in range(PACK):
-            second(accs[t], 0, t, z_codes[:], z_scales[:], t != 3, False)
+            second(accs[t], 1, t, g_codes[:], g_scales[:], t != 3, False)
         for t in range(PACK):
-            second(accs[t], 1, t, g_codes[:], g_scales[:], False, t != 2)
+            second(accs[t], 0, t, z_codes[:], z_scales[:], False, t != 2)
         for t in range(2):
             nc.scalar.copy(y_second[:, t, :], accs[t])
         nc.sync.dma_start(out_rows[:, 0:2, HV:V], y_second[:, 0:2, :])

@@ -62,10 +62,9 @@ def tile_picked_sagecat_mean_lo_kernel(
         offs_sb = sb.tile([P, S // 16], U16, name="offs_sb")
         x_rows = xT.rearrange("(p j) n -> p j n", j=PACK)
         x_raw = [sbuf("x_raw%d" % j, [P, T], F32) for j in range(PACK)]
+        nc.sync.dma_start(offs_sb[:], offs)
         for j in range(PACK):
             nc.sync.dma_start(x_raw[j][:], x_rows[:, j, :])
-            if j == 0:
-                nc.sync.dma_start(offs_sb[:], offs)
         w1_raw = sbuf("w1_raw", [P, PACK, H], F32)
         nc.sync.dma_start(w1_raw[:], w1.rearrange("(p j) c -> p j c", j=PACK))
         lists = []
@@ -76,11 +75,11 @@ def tile_picked_sagecat_mean_lo_kernel(
         cen_sb = lists[4]
         w_raw = []
         for number, w in enumerate((w3, w2)):
-            raw = sbuf("w_raw%d" % number, [P, PACK, H], F32)
-            rows = w.rearrange("(u t b) c -> b u t c", t=PACK, b=4)
-            for b in range(4):
-                nc.sync.dma_start(raw[b:P:4, :, :], rows[b])
-            w_raw.append(raw)
+            rows = w.rearrange("(p j) c -> p j c", j=PACK)
+            for e in range(2):
+                raw = sbuf("w_raw%d" % (2 * number + e), [P, PACK, H // 2], F32)
+                nc.sync.dma_start(raw[:], rows[:, :, e * H // 2 : (e + 1) * H // 2])
+                w_raw.append(raw)
 
         def half_of(list_sb, half, entries):
             return list_sb[:, half * entries // 16 : (half + 1) * entries // 16]
@@ -94,7 +93,11 @@ def tile_picked_sagecat_mean_lo_kernel(
         x_found = [sbuf("x_found%d" % a, [P, PACK, HS], F32) for a in range(2)]
         for j in range(PACK):
             nc.vector.tensor_copy(x_found[0][:, j, :], x_raw[j][:].indirect(half_of(offs_sb, 0, HS)))
-            fetch(x_found[1][:, j, :], x_raw[j][:], half_of(offs_sb, 1, HS))
+            if j < 2:
+                nc.vector.tensor_copy(x_found[1][:, j, 0:P], x_raw[j][:].indirect(half_of(offs_sb, 2, P)))
+                fetch(x_found[1][:, j, P:HS], x_raw[j][:], half_of(offs_sb, 3, P))
+            else:
+                fetch(x_found[1][:, j, :], x_raw[j][:], half_of(offs_sb, 1, HS))
         nc.scalar.copy(woven(x_bf[1][:, 0:P, :]), planes(x_found[1][:, :, 0:P]))
         for q in range(2):
             nc.vector.tensor_copy(woven(x_bf[0][:, q * P : (q + 1) * P, :]), planes(x_found[0][:, :, q * P : (q + 1) * P]))
@@ -103,18 +106,19 @@ def tile_picked_sagecat_mean_lo_kernel(
             cols = slice(a * HS, (a + 1) * HS)
             quantize(x_codes[:, cols], x_scales[:, cols], x_bf[a][:])
 
-        w1_dealt = w1_raw[:].rearrange("p j (u t b) -> p t u j b", t=PACK, b=4)
+        w1_dealt = w1_raw[:].rearrange("p j (e m u t) -> p u e m j t", e=2, u=2, t=2)
         h = [sbuf("h%d" % t, [P, S], F32) for t in range(PACK)]
         w1_bf = []
-        for t in range(PACK):
-            rounded = sbuf("w1_bf%d" % t, [P, P, PACK], BF16)
-            cast = nc.scalar.copy if t in (0, 3) else nc.vector.tensor_copy
-            cast(rounded[:].rearrange("p (u b) j -> p u j b", b=4), w1_dealt[:, t])
-            w1_bf.append(rounded)
+        for u in range(2):
+            rounded = sbuf("w1_bf%d" % u, [P, 2, P, PACK], BF16)
+            dealt = rounded[:].rearrange("p t (e m) j -> p e m j t", e=2)
+            nc.vector.tensor_copy(dealt[:, 0], w1_dealt[:, u, 0])
+            nc.scalar.copy(dealt[:, 1], w1_dealt[:, u, 1])
+            w1_bf.extend([rounded[:, 0], rounded[:, 1]])
         for t in range(PACK):
             w1_codes = sbuf("w1_codes%d" % t, [P, P], U32)
             w1_scales = sbuf("w1_scales%d" % t, [P, P], U8)
-            quantize(w1_codes[:], w1_scales[:], w1_bf[t][:])
+            quantize(w1_codes[:], w1_scales[:], w1_bf[t])
             if t == 0:
                 for a in range(2):
                     cols = slice(a * HS, (a + 1) * HS)
@@ -133,29 +137,27 @@ def tile_picked_sagecat_mean_lo_kernel(
         w_scales = sbuf("w_scales", [P, 2 * H], U8)
 
         def second_weights(number):
-            w_bf = [sbuf("w_bf%d_%d" % (number, e), [P, H // 2, PACK], BF16) for e in range(2)]
-            src = w_raw[number][:].rearrange("p j (m e t) -> p e m j t", e=2, t=2)
+            w_bf = sbuf("w_bf%d" % number, [P, H, PACK], BF16)
+            dealt = w_bf[:].rearrange("p (t e m) j -> p e m j t", t=PACK, e=2)
             for e in range(2):
-                nc.vector.tensor_copy(w_bf[e][:].rearrange("p (t m) j -> p m j t", t=2), src[:, e])
-            for e in range(2):
-                cols = slice(number * H + e * H // 2, number * H + (e + 1) * H // 2)
-                quantize(w_codes[:, cols], w_scales[:, cols], w_bf[e][:])
+                src = w_raw[2 * number + e][:].rearrange("p j (m t) -> p m j t", t=PACK)
+                nc.vector.tensor_copy(dealt[:, e], src)
+            cols = slice(number * H, (number + 1) * H)
+            quantize(w_codes[:, cols], w_scales[:, cols], w_bf[:])
 
         def second(acc, number, t, codes, scales, start, stop):
             m = slice(number * H + t * P, number * H + (t + 1) * P)
             multiply(acc, w_codes[:, m], w_scales[:, m], codes, scales, start, stop)
 
-        def fetch_all(name, list_sb, a, factor=1.0, tag=None):
-            found = sbuf(name, [P, PACK, HV], F32, tag=tag)
+        def fetch_all(name, offsets, width, factor=1.0, tag=None):
+            found = sbuf(name, [P, PACK, width], F32, tag=tag)
             for t in range(PACK):
-                fetch(found[:, t, :], h[t][:], half_of(list_sb, a, HV), factor)
+                fetch(found[:, t, :], h[t][:], offsets, factor)
             return found
 
-        def add_all(name, list_sb, a, earlier, tag=None):
-            total = sbuf(name, [P, PACK, HV], F32, tag=tag)
+        def add_all(total, offsets, earlier):
             for t in range(PACK):
-                nc.vector.tensor_tensor(total[:, t, :], h[t][:].indirect(half_of(list_sb, a, HV)), earlier[:, t, :], ADD)
-            return total
+                nc.vector.tensor_tensor(total[:, t, :], h[t][:].indirect(offsets), earlier[:, t, :], ADD)
 
         def join(z_bf, left, right):
             nc.vector.tensor_tensor(
@@ -175,15 +177,17 @@ def tile_picked_sagecat_mean_lo_kernel(
             quantize(y_codes[:, cols], y_scales[:, cols], y_bf[:])
 
         second_weights(0)
-        one = fetch_all("one0", lists[0], 0)
-        two = add_all("two0", lists[1], 0, one, tag="w_raw0")
+        one = fetch_all("one", lists[0][:], V)
+        two = sbuf("two", [P, PACK, V], F32, tag="w_raw1")
         second_weights(1)
-        three = fetch_all("three0", lists[2], 0)
-        four = add_all("four0", lists[3], 0, three, tag="w_raw1")
-        centres = fetch_all("centres0", cen_sb, 0, 4.0)
+        add_all(two[:], lists[1][:], one[:])
+        three = fetch_all("three0", half_of(lists[2], 0, HV), HV, tag="w1_codes3")
+        four = sbuf("four", [P, 2, PACK, HV], F32, tag="w_raw3")
+        add_all(four[:, 0], half_of(lists[3], 0, HV), three[:])
+        centres = fetch_all("centres0", half_of(cen_sb, 0, HV), HV, 4.0, tag="w1_scales3")
         zg_bf = sbuf("zg_bf", [P, 2, HV, PACK], BF16)
         nc.scalar.copy(woven(zg_bf[:, 1]), planes(centres[:]))
-        join(zg_bf[:, 0], two[:], four[:])
+        join(zg_bf[:, 0], two[:, :, 0:HV], four[:, 0])
         zg_codes = sbuf("zg_codes", [P, V], U32)
         zg_scales = sbuf("zg_scales", [P, V], U8)
         quantize(zg_codes[:], zg_scales[:], zg_bf[:].rearrange("p n c t -> p (n c) t"))
@@ -193,27 +197,25 @@ def tile_picked_sagecat_mean_lo_kernel(
                 cols = slice(number * HV, (number + 1) * HV)
                 second(whole[:, t, :], number, t, zg_codes[:, cols], zg_scales[:, cols], number == 0, number == 1)
 
-        one = fetch_all("one1", lists[0], 1, tag="w1_codes3")
-        two = add_all("two1", lists[1], 1, one, tag="three0")
-        three = fetch_all("three1", lists[2], 1, tag="w1_scales3")
-        four = add_all("four1", lists[3], 1, three, tag="w_raw0")
-        centres = fetch_all("centres1", cen_sb, 1, 4.0, tag="x_codes")
-        g_bf = sbuf("g_bf", [P, HV, PACK], BF16, tag="w1_codes3")
-        nc.vector.tensor_copy(woven(g_bf[:]), planes(centres[:]))
+        three = fetch_all("three1", half_of(lists[2], 1, HV), HV, tag="x_codes")
+        add_all(four[:, 1], half_of(lists[3], 1, HV), three[:])
+        centres = fetch_all("centres1", half_of(cen_sb, 1, HV), HV, 4.0, tag="x_scales")
         z_bf = sbuf("z_bf", [P, HV, PACK], BF16)
-        join(z_bf[:], two[:], four[:])
-        g_codes = sbuf("g_codes", [P, HV], U32)
-        g_scales = sbuf("g_scales", [P, HV], U8)
-        quantize(g_codes[:], g_scales[:], g_bf[:])
+        join(z_bf[:], two[:, :, HV:V], four[:, 1])
+        g_bf = sbuf("g_bf", [P, HV, PACK], BF16, tag="zg_bf")
+        nc.vector.tensor_copy(woven(g_bf[:]), planes(centres[:]))
         z_codes = sbuf("z_codes", [P, HV], U32)
         z_scales = sbuf("z_scales", [P, HV], U8)
         quantize(z_codes[:], z_scales[:], z_bf[:])
+        g_codes = sbuf("g_codes", [P, HV], U32)
+        g_scales = sbuf("g_scales", [P, HV], U8)
+        quantize(g_codes[:], g_scales[:], g_bf[:])
 
-        y_first = sbuf("y_first", [P, PACK, HV], F32)
+        y_first = sbuf("y_first", [P, PACK, HV], F32, tag="x_scales")
         nc.scalar.copy(y_first[:], whole[:])
         nc.sync.dma_start(out_rows[:, :, 0:HV], y_first[:])
-        y_first_bf = sbuf("y_first_bf", [P, HV, PACK], BF16)
-        nc.scalar.copy(woven(y_first_bf[:]), planes(y_first[:]))
+        y_first_bf = sbuf("y_first_bf", [P, HV, PACK], BF16, tag="zg_bf")
+        nc.vector.tensor_copy(woven(y_first_bf[:]), planes(y_first[:]))
         hand_out(0, y_first_bf)
 
         y_second = sbuf("y_second", [P, PACK, HV], F32)
@@ -221,9 +223,9 @@ def tile_picked_sagecat_mean_lo_kernel(
         last_pair = bank(6, "y_acc_pair", [P, 2, HV])
         accs = [bank(7, "y_acc0", [P, HV])[:], bank(0, "y_acc1", [P, HV])[:], last_pair[:, 0, :], last_pair[:, 1, :]]
         for t in range(PACK):
-            second(accs[t], 1, t, g_codes[:], g_scales[:], t != 3, False)
+            second(accs[t], 0, t, z_codes[:], z_scales[:], t != 3, False)
         for t in range(PACK):
-            second(accs[t], 0, t, z_codes[:], z_scales[:], False, t != 2)
+            second(accs[t], 1, t, g_codes[:], g_scales[:], False, t != 2)
         for t in range(2):
             nc.scalar.copy(y_second[:, t, :], accs[t])
         nc.sync.dma_start(out_rows[:, 0:2, HV:V], y_second[:, 0:2, :])

@@ -136,14 +136,17 @@ def tile_picked_sagecat_mean_lo_kernel(
         w_codes = sbuf("w_codes", [P, 2 * H], U32)
         w_scales = sbuf("w_scales", [P, 2 * H], U8)
 
-        def second_weights(number):
-            w_bf = sbuf("w_bf%d" % number, [P, H, PACK], BF16)
-            dealt = w_bf[:].rearrange("p (t e m) j -> p e m j t", t=PACK, e=2)
-            for e in range(2):
-                src = w_raw[2 * number + e][:].rearrange("p j (m t) -> p m j t", t=PACK)
-                nc.vector.tensor_copy(dealt[:, e], src)
-            cols = slice(number * H, (number + 1) * H)
-            quantize(w_codes[:, cols], w_scales[:, cols], w_bf[:])
+        w_bf = [[sbuf("w_bf%d_%d" % (number, u), [P, 2, P, PACK], BF16) for u in range(2)] for number in range(2)]
+
+        def round_weights(number, e):
+            src = w_raw[2 * number + e][:].rearrange("p j (m u t) -> p u m j t", u=2, t=2)
+            for u in range(2):
+                nc.vector.tensor_copy(w_bf[number][u][:].rearrange("p t (e m) j -> p e m j t", e=2)[:, e], src[:, u])
+
+        def quantize_weights(number):
+            for u in range(2):
+                cols = slice(number * H + u * H // 2, number * H + (u + 1) * H // 2)
+                quantize(w_codes[:, cols], w_scales[:, cols], w_bf[number][u][:].rearrange("p t m j -> p (t m) j"))
 
         def second(acc, number, t, codes, scales, start, stop):
             m = slice(number * H + t * P, number * H + (t + 1) * P)
@@ -176,11 +179,15 @@ def tile_picked_sagecat_mean_lo_kernel(
             cols = slice(a * HV, (a + 1) * HV)
             quantize(y_codes[:, cols], y_scales[:, cols], y_bf[:])
 
-        second_weights(0)
+        round_weights(0, 0)
+        round_weights(0, 1)
+        quantize_weights(0)
+        round_weights(1, 0)
         one = fetch_all("one", lists[0][:], V)
-        two = sbuf("two", [P, PACK, V], F32, tag="w_raw1")
-        second_weights(1)
+        two = sbuf("two", [P, PACK, V], F32, tag="w_raw2")
         add_all(two[:], lists[1][:], one[:])
+        round_weights(1, 1)
+        quantize_weights(1)
         three = fetch_all("three0", half_of(lists[2], 0, HV), HV, tag="w1_codes3")
         four = sbuf("four", [P, 2, PACK, HV], F32, tag="w_raw3")
         add_all(four[:, 0], half_of(lists[3], 0, HV), three[:])

@@ -13,8 +13,6 @@ U16 = mybir.dt.uint16
 U8 = mybir.dt.uint8
 FP8X4 = mybir.dt.float8_e4m3fn_x4
 ADD = mybir.AluOpType.add
-MAX = mybir.AluOpType.max
-MULT = mybir.AluOpType.mult
 COPY = mybir.ActivationFunctionType.Copy
 RELU = mybir.ActivationFunctionType.Relu
 
@@ -112,7 +110,8 @@ def tile_picked_sagecat_mean_lo_kernel(
         for u in range(2):
             rounded = sbuf("w1_bf%d" % u, [P, 2, P, PACK], BF16)
             dealt = rounded[:].rearrange("p t (e m) j -> p e m j t", e=2)
-            nc.vector.tensor_copy(dealt[:, 0], w1_dealt[:, u, 0])
+            first_cast = nc.vector.tensor_copy if u == 0 else nc.scalar.copy
+            first_cast(dealt[:, 0], w1_dealt[:, u, 0])
             nc.scalar.copy(dealt[:, 1], w1_dealt[:, u, 1])
             w1_bf.extend([rounded[:, 0], rounded[:, 1]])
         for t in range(PACK):
@@ -124,10 +123,7 @@ def tile_picked_sagecat_mean_lo_kernel(
                     cols = slice(a * HS, (a + 1) * HS)
                     acc = bank(a, "h0_acc%d" % a, [P, HS])
                     multiply(acc[:], w1_codes[:], w1_scales[:], x_codes[:, cols], x_scales[:, cols], True, True)
-                    if a == 0:
-                        nc.vector.tensor_scalar(h[0][:, cols], acc[:], 0.0, 0.25, MAX, MULT)
-                    else:
-                        nc.scalar.activation(h[0][:, cols], acc[:], RELU, scale=0.25)
+                    nc.scalar.activation(h[0][:, cols], acc[:], RELU, scale=0.25)
             else:
                 acc = bank(1 + t, "h_acc%d" % t, [P, S])
                 multiply(acc[:], w1_codes[:], w1_scales[:], x_codes[:], x_scales[:], True, True)

@@ -71,13 +71,13 @@ def tile_picked_sagecat_mean_lo_kernel(
             nc.sync.dma_start(list_sb[:], src)
             lists.append(list_sb)
         cen_sb = lists[4]
-        w_raw = []
+        w2_raw = sbuf("w2_raw", [P, 2 * PACK, H // 2], F32)
+        w_raw = [sbuf("w_raw%d" % e, [P, PACK, H // 2], F32)[:] for e in range(2)]
+        w_raw.extend([w2_raw[:, 0:PACK, :], w2_raw[:, PACK : 2 * PACK, :]])
         for number, w in enumerate((w3, w2)):
             rows = w.rearrange("(p j) c -> p j c", j=PACK)
             for e in range(2):
-                raw = sbuf("w_raw%d" % (2 * number + e), [P, PACK, H // 2], F32)
-                nc.sync.dma_start(raw[:], rows[:, :, e * H // 2 : (e + 1) * H // 2])
-                w_raw.append(raw)
+                nc.sync.dma_start(w_raw[2 * number + e], rows[:, :, e * H // 2 : (e + 1) * H // 2])
 
         def half_of(list_sb, half, entries):
             return list_sb[:, half * entries // 16 : (half + 1) * entries // 16]
@@ -114,30 +114,35 @@ def tile_picked_sagecat_mean_lo_kernel(
             first_cast(dealt[:, 0], w1_dealt[:, u, 0])
             nc.scalar.copy(dealt[:, 1], w1_dealt[:, u, 1])
             w1_bf.extend([rounded[:, 0], rounded[:, 1]])
+        w_bf = [[sbuf("w_bf%d_%d" % (number, u), [P, 2, P, PACK], BF16) for u in range(2)] for number in range(2)]
+
+        def round_weights(number, e):
+            src = w_raw[2 * number + e].rearrange("p j (m u t) -> p u m j t", u=2, t=2)
+            for u in range(2):
+                nc.vector.tensor_copy(w_bf[number][u][:].rearrange("p t (e m) j -> p e m j t", e=2)[:, e], src[:, u])
+
+        pair_codes = []
         for t in range(PACK):
-            w1_codes = sbuf("w1_codes%d" % t, [P, P], U32)
+            if t == 2:
+                round_weights(0, 0)
+            if t % 2 == 0:
+                pair_codes.append(sbuf("w1_codes%d" % (t + 1), [P, 2, P], U32, tag="w_raw0" if t == 2 else None))
+            w1_codes = pair_codes[t // 2][:, t % 2]
             w1_scales = sbuf("w1_scales%d" % t, [P, P], U8)
-            quantize(w1_codes[:], w1_scales[:], w1_bf[t])
+            quantize(w1_codes, w1_scales[:], w1_bf[t])
             if t == 0:
                 for a in range(2):
                     cols = slice(a * HS, (a + 1) * HS)
                     acc = bank(a, "h0_acc%d" % a, [P, HS])
-                    multiply(acc[:], w1_codes[:], w1_scales[:], x_codes[:, cols], x_scales[:, cols], True, True)
+                    multiply(acc[:], w1_codes, w1_scales[:], x_codes[:, cols], x_scales[:, cols], True, True)
                     nc.scalar.activation(h[0][:, cols], acc[:], RELU, scale=0.25)
             else:
                 acc = bank(1 + t, "h_acc%d" % t, [P, S])
-                multiply(acc[:], w1_codes[:], w1_scales[:], x_codes[:], x_scales[:], True, True)
+                multiply(acc[:], w1_codes, w1_scales[:], x_codes[:], x_scales[:], True, True)
                 nc.scalar.activation(h[t][:], acc[:], RELU, scale=0.25)
 
         w_codes = sbuf("w_codes", [P, 2 * H], U32)
         w_scales = sbuf("w_scales", [P, 2 * H], U8)
-
-        w_bf = [[sbuf("w_bf%d_%d" % (number, u), [P, 2, P, PACK], BF16) for u in range(2)] for number in range(2)]
-
-        def round_weights(number, e):
-            src = w_raw[2 * number + e][:].rearrange("p j (m u t) -> p u m j t", u=2, t=2)
-            for u in range(2):
-                nc.vector.tensor_copy(w_bf[number][u][:].rearrange("p t (e m) j -> p e m j t", e=2)[:, e], src[:, u])
 
         def quantize_weights(number):
             for u in range(2):
@@ -175,17 +180,18 @@ def tile_picked_sagecat_mean_lo_kernel(
             cols = slice(a * HV, (a + 1) * HV)
             quantize(y_codes[:, cols], y_scales[:, cols], y_bf[:])
 
-        round_weights(0, 0)
         round_weights(0, 1)
+        one = fetch_all("one", lists[0][:], V)
         quantize_weights(0)
         round_weights(1, 0)
-        one = fetch_all("one", lists[0][:], V)
-        two = sbuf("two", [P, PACK, V], F32, tag="w_raw2")
-        add_all(two[:], lists[1][:], one[:])
-        round_weights(1, 1)
-        quantize_weights(1)
-        three = fetch_all("three0", half_of(lists[2], 0, HV), HV, tag="w1_codes3")
-        four = sbuf("four", [P, 2, PACK, HV], F32, tag="w_raw3")
+        two = w2_raw[:, 2 : 2 + PACK, :]
+        for t in range(PACK):
+            if t == 2:
+                round_weights(1, 1)
+                quantize_weights(1)
+            nc.vector.tensor_tensor(two[:, t, :], h[t][:].indirect(lists[1][:]), one[:, t, :], ADD)
+        three = fetch_all("three0", half_of(lists[2], 0, HV), HV, tag="w_raw0")
+        four = sbuf("four", [P, 2, PACK, HV], F32, tag="w_bf1_1")
         add_all(four[:, 0], half_of(lists[3], 0, HV), three[:])
         centres = fetch_all("centres0", half_of(cen_sb, 0, HV), HV, 4.0, tag="w1_scales3")
         zg_bf = sbuf("zg_bf", [P, 2, HV, PACK], BF16)

@@ -60,9 +60,10 @@ def tile_picked_sagecat_mean_lo_kernel(
         offs_sb = sb.tile([P, S // 16], U16, name="offs_sb")
         x_rows = xT.rearrange("(p j) n -> p j n", j=PACK)
         x_raw = [sbuf("x_raw%d" % j, [P, T], F32) for j in range(PACK)]
-        nc.sync.dma_start(offs_sb[:], offs)
         for j in range(PACK):
             nc.sync.dma_start(x_raw[j][:], x_rows[:, j, :])
+            if j == 0:
+                nc.sync.dma_start(offs_sb[:], offs)
         w1_raw = sbuf("w1_raw", [P, PACK, H], F32)
         nc.sync.dma_start(w1_raw[:], w1.rearrange("(p j) c -> p j c", j=PACK))
         lists = []
@@ -90,29 +91,40 @@ def tile_picked_sagecat_mean_lo_kernel(
         x_bf = [sbuf("x_bf%d" % a, [P, HS, PACK], BF16) for a in range(2)]
         x_found = [sbuf("x_found%d" % a, [P, PACK, HS], F32) for a in range(2)]
         for j in range(PACK):
-            nc.vector.tensor_copy(x_found[0][:, j, :], x_raw[j][:].indirect(half_of(offs_sb, 0, HS)))
+            if j < PACK - 1:
+                nc.vector.tensor_copy(x_found[0][:, j, :], x_raw[j][:].indirect(half_of(offs_sb, 0, HS)))
+            else:
+                for q in range(2):
+                    nc.vector.tensor_copy(x_found[0][:, j, q * P : (q + 1) * P], x_raw[j][:].indirect(half_of(offs_sb, q, P)))
             if j < 2:
                 nc.vector.tensor_copy(x_found[1][:, j, 0:P], x_raw[j][:].indirect(half_of(offs_sb, 2, P)))
                 fetch(x_found[1][:, j, P:HS], x_raw[j][:], half_of(offs_sb, 3, P))
-            else:
+            elif j == 2:
                 fetch(x_found[1][:, j, :], x_raw[j][:], half_of(offs_sb, 1, HS))
-        nc.scalar.copy(woven(x_bf[1][:, 0:P, :]), planes(x_found[1][:, :, 0:P]))
-        for q in range(2):
-            nc.vector.tensor_copy(woven(x_bf[0][:, q * P : (q + 1) * P, :]), planes(x_found[0][:, :, q * P : (q + 1) * P]))
-        nc.vector.tensor_copy(woven(x_bf[1][:, P:HS, :]), planes(x_found[1][:, :, P:HS]))
+            else:
+                for q in range(2):
+                    fetch(x_found[1][:, j, q * P : (q + 1) * P], x_raw[j][:], half_of(offs_sb, 2 + q, P))
+        for first, last, weave, a in (
+            (0, 128, nc.scalar.copy, 1),
+            (128, 192, nc.scalar.copy, 1),
+            (0, 128, nc.vector.tensor_copy, 0),
+            (128, 256, nc.vector.tensor_copy, 0),
+            (192, 256, nc.vector.tensor_copy, 1),
+        ):
+            weave(woven(x_bf[a][:, first:last, :]), planes(x_found[a][:, :, first:last]))
         for a in range(2):
             cols = slice(a * HS, (a + 1) * HS)
             quantize(x_codes[:, cols], x_scales[:, cols], x_bf[a][:])
 
-        w1_dealt = w1_raw[:].rearrange("p j (e m u t) -> p u e m j t", e=2, u=2, t=2)
+        w1_dealt = w1_raw[:].rearrange("p j (m u t) -> p u m j t", u=2, t=2)
         h = [sbuf("h%d" % t, [P, S], F32) for t in range(PACK)]
         w1_bf = []
         for u in range(2):
             rounded = sbuf("w1_bf%d" % u, [P, 2, P, PACK], BF16)
-            dealt = rounded[:].rearrange("p t (e m) j -> p e m j t", e=2)
-            first_cast = nc.vector.tensor_copy if u == 0 else nc.scalar.copy
-            first_cast(dealt[:, 0], w1_dealt[:, u, 0])
-            nc.scalar.copy(dealt[:, 1], w1_dealt[:, u, 1])
+            dealt = rounded[:].rearrange("p t m j -> p m j t")
+            share = (80, 32)[u]
+            nc.vector.tensor_copy(dealt[:, 0:share], w1_dealt[:, u, 0:share])
+            nc.scalar.copy(dealt[:, share:P], w1_dealt[:, u, share:P])
             w1_bf.extend([rounded[:, 0], rounded[:, 1]])
         w_bf = [[sbuf("w_bf%d_%d" % (number, u), [P, 2, P, PACK], BF16) for u in range(2)] for number in range(2)]
 
@@ -190,9 +202,9 @@ def tile_picked_sagecat_mean_lo_kernel(
                 round_weights(1, 1)
                 quantize_weights(1)
             nc.vector.tensor_tensor(two[:, t, :], h[t][:].indirect(lists[1][:]), one[:, t, :], ADD)
-        three = fetch_all("three0", half_of(lists[2], 0, HV), HV, tag="w_raw0")
+        three = fetch_all("three", lists[2][:], V, tag="w_raw0")
         four = sbuf("four", [P, 2, PACK, HV], F32, tag="w_bf1_1")
-        add_all(four[:, 0], half_of(lists[3], 0, HV), three[:])
+        add_all(four[:, 0], half_of(lists[3], 0, HV), three[:, :, 0:HV])
         centres = fetch_all("centres0", half_of(cen_sb, 0, HV), HV, 4.0, tag="w1_scales3")
         zg_bf = sbuf("zg_bf", [P, 2, HV, PACK], BF16)
         nc.scalar.copy(woven(zg_bf[:, 1]), planes(centres[:]))
@@ -206,8 +218,7 @@ def tile_picked_sagecat_mean_lo_kernel(
                 cols = slice(number * HV, (number + 1) * HV)
                 second(whole[:, t, :], number, t, zg_codes[:, cols], zg_scales[:, cols], number == 0, number == 1)
 
-        three = fetch_all("three1", half_of(lists[2], 1, HV), HV, tag="x_codes")
-        add_all(four[:, 1], half_of(lists[3], 1, HV), three[:])
+        add_all(four[:, 1], half_of(lists[3], 1, HV), three[:, :, HV:V])
         centres = fetch_all("centres1", half_of(cen_sb, 1, HV), HV, 4.0, tag="x_scales")
         z_bf = sbuf("z_bf", [P, HV, PACK], BF16)
         join(z_bf[:], two[:, :, HV:V], four[:, 1])

@@ -67,18 +67,22 @@ def tile_picked_sagecat_mean_lo_kernel(
         w1_raw = sbuf("w1_raw", [P, PACK, H], F32)
         nc.sync.dma_start(w1_raw[:], w1.rearrange("(p j) c -> p j c", j=PACK))
         lists = []
-        for number, src in enumerate((pos1, pos2, pos3, pos4, cen)):
-            list_sb = sb.tile([P, V // 16], U16, name="list%d" % number)
-            nc.sync.dma_start(list_sb[:], src)
-            lists.append(list_sb)
-        cen_sb = lists[4]
-        w2_raw = sbuf("w2_raw", [P, 2 * PACK, H // 2], F32)
-        w_raw = [sbuf("w_raw%d" % e, [P, PACK, H // 2], F32)[:] for e in range(2)]
-        w_raw.extend([w2_raw[:, 0:PACK, :], w2_raw[:, PACK : 2 * PACK, :]])
+
+        def load_lists(sources):
+            for src in sources:
+                list_sb = sb.tile([P, V // 16], U16, name="list%d" % len(lists))
+                nc.sync.dma_start(list_sb[:], src)
+                lists.append(list_sb)
+
+        load_lists([pos1, pos2, pos3])
+        rows_sb = sbuf("rows_sb", [P, 16, H // 2], F32)
+        w_raw = [sbuf("w_raw0", [P, PACK, H // 2], F32)[:], rows_sb[:, 0:4, :], rows_sb[:, 4:8, :], rows_sb[:, 9:16:2, :]]
         for number, w in enumerate((w3, w2)):
             rows = w.rearrange("(p j) c -> p j c", j=PACK)
             for e in range(2):
                 nc.sync.dma_start(w_raw[2 * number + e], rows[:, :, e * H // 2 : (e + 1) * H // 2])
+        load_lists([pos4, cen])
+        cen_sb = lists[4]
 
         def half_of(list_sb, half, entries):
             return list_sb[:, half * entries // 16 : (half + 1) * entries // 16]
@@ -192,12 +196,19 @@ def tile_picked_sagecat_mean_lo_kernel(
             cols = slice(a * HV, (a + 1) * HV)
             quantize(y_codes[:, cols], y_scales[:, cols], y_bf[:])
 
+        def quantize_w3(e):
+            for t in range(PACK):
+                cols = slice(t * P + e * P // 2, t * P + (e + 1) * P // 2)
+                quantize(w_codes[:, cols], w_scales[:, cols], w_bf[0][t // 2][:, t % 2, e * P // 2 : (e + 1) * P // 2, :])
+
+        quantize_w3(0)
         round_weights(0, 1)
         one = fetch_all("one", lists[0][:], V)
-        quantize_weights(0)
-        round_weights(1, 0)
-        two = w2_raw[:, 2 : 2 + PACK, :]
+        quantize_w3(1)
+        two = rows_sb[:, 3:16:4, :]
         for t in range(PACK):
+            if t == 1:
+                round_weights(1, 0)
             if t == 2:
                 round_weights(1, 1)
                 quantize_weights(1)

@@ -74,10 +74,12 @@ def tile_picked_sagecat_mean_lo_kernel(
                 nc.sync.dma_start(list_sb[:], src)
                 lists.append(list_sb)
 
-        load_lists([pos1, pos2, pos3])
+        load_lists([pos1])
         rows_sb = sbuf("rows_sb", [P, 16, H // 2], F32)
         w_raw = [sbuf("w_raw0", [P, PACK, H // 2], F32)[:], rows_sb[:, 0:4, :], rows_sb[:, 4:8, :], rows_sb[:, 9:16:2, :]]
         for number, w in enumerate((w3, w2)):
+            if number == 1:
+                load_lists([pos2, pos3])
             rows = w.rearrange("(p j) c -> p j c", j=PACK)
             for e in range(2):
                 nc.sync.dma_start(w_raw[2 * number + e], rows[:, :, e * H // 2 : (e + 1) * H // 2])
@@ -181,9 +183,9 @@ def tile_picked_sagecat_mean_lo_kernel(
 
         def join(z_bf, left, right):
             nc.vector.tensor_tensor(
-                z_bf.rearrange("p (c i) t -> p c t i", i=2),
-                left.rearrange("p t (c i) -> p c t i", i=2),
-                right.rearrange("p t (c i) -> p c t i", i=2),
+                woven(z_bf),
+                planes(left),
+                planes(right),
                 ADD,
             )
 

@@ -52,7 +52,7 @@ def tile_picked_sagecat_mean_lo_kernel(
         psum = ctx.enter_context(tc.psum_pool(name="psum", bufs=1))
 
         def sbuf(name, shape, dtype, tag=None):
-            return sb.tile(shape, dtype, name=name, tag=tag or name, align_bytes=64)
+            return sb.tile(shape, dtype, name=name, tag=tag or name, align_bytes=256)
 
         def bank(number, name, shape):
             return psum.tile(shape, F32, name=name, tag="bank%d" % number)

@@ -49,10 +49,14 @@ def tile_picked_sagecat_mean_lo_kernel(
 
     with ExitStack() as ctx:
         sb = ctx.enter_context(tc.tile_pool(name="sb", bufs=1))
+        placed = ctx.enter_context(tc.tile_pool(name="placed", bufs=1))
         psum = ctx.enter_context(tc.psum_pool(name="psum", bufs=1))
 
         def sbuf(name, shape, dtype, tag=None):
             return sb.tile(shape, dtype, name=name, tag=tag or name, align_bytes=256)
+
+        def place(name, shape, dtype, kib):
+            return placed.tile(shape, dtype, name=name, align_bytes=256, offset=kib * 1024)
 
         def bank(number, name, shape):
             return psum.tile(shape, F32, name=name, tag="bank%d" % number)
@@ -75,16 +79,16 @@ def tile_picked_sagecat_mean_lo_kernel(
                 lists.append(list_sb)
 
         load_lists([pos1])
-        rows_sb = sbuf("rows_sb", [P, 16, H // 2], F32)
-        w_raw = [sbuf("w_raw0", [P, PACK, H // 2], F32)[:], rows_sb[:, 0:4, :], rows_sb[:, 4:8, :], rows_sb[:, 9:16:2, :]]
+        w_raw = [sbuf("w_raw0", [P, PACK, H // 2], F32)[:]]
+        w_raw.extend([place("w_raw%d" % n, [P, PACK, H // 2], F32, kib)[:] for n, kib in ((1, 0), (2, 4), (3, 12))])
         for number, w in enumerate((w3, w2)):
             if number == 1:
-                load_lists([pos2, pos3])
+                load_lists([pos2, cen])
             rows = w.rearrange("(p j) c -> p j c", j=PACK)
             for e in range(2):
                 nc.sync.dma_start(w_raw[2 * number + e], rows[:, :, e * H // 2 : (e + 1) * H // 2])
-        load_lists([pos4, cen])
-        cen_sb = lists[4]
+        load_lists([pos4, pos3])
+        cen_sb, fourth_sb, third_sb = lists[2:5]
 
         def half_of(list_sb, half, entries):
             return list_sb[:, half * entries // 16 : (half + 1) * entries // 16]
@@ -132,13 +136,18 @@ def tile_picked_sagecat_mean_lo_kernel(
             nc.vector.tensor_copy(dealt[:, 0:share], w1_dealt[:, u, 0:share])
             nc.scalar.copy(dealt[:, share:P], w1_dealt[:, u, share:P])
             w1_bf.extend([rounded[:, 0], rounded[:, 1]])
-        w_bf = [[sbuf("w_bf%d_%d" % (number, u), [P, 2, P, PACK], BF16) for u in range(2)] for number in range(2)]
+        w_bf = [sbuf("w_bf%d" % number, [P, PACK, P, PACK], BF16) for number in range(2)]
 
         def round_weights(number, e):
             src = w_raw[2 * number + e].rearrange("p j (m u t) -> p u m j t", u=2, t=2)
-            for u in range(2):
-                nc.vector.tensor_copy(w_bf[number][u][:].rearrange("p t (e m) j -> p e m j t", e=2)[:, e], src[:, u])
+            dst = w_bf[number][:].rearrange("p (u t) (e m) j -> p e u m j t", u=2, e=2)[:, e]
+            if (number, e) == (0, 1):
+                for u in range(2):
+                    nc.vector.tensor_copy(dst[:, u], src[:, u])
+            else:
+                nc.vector.tensor_copy(dst, src)
 
+        one = sbuf("one", [P, PACK, V], F32)
         pair_codes = []
         for t in range(PACK):
             if t == 2:
@@ -158,28 +167,26 @@ def tile_picked_sagecat_mean_lo_kernel(
                 acc = bank(1 + t, "h_acc%d" % t, [P, S])
                 multiply(acc[:], w1_codes, w1_scales[:], x_codes[:], x_scales[:], True, True)
                 nc.scalar.activation(h[t][:], acc[:], RELU, scale=0.25)
+            fetch(one[:, t, :], h[t][:], lists[0][:])
 
-        w_codes = sbuf("w_codes", [P, 2 * H], U32)
+        w_codes = sbuf("w_codes", [P, H + H // 2], U32)
         w_scales = sbuf("w_scales", [P, 2 * H], U8)
 
-        def quantize_weights(number):
-            for u in range(2):
-                cols = slice(number * H + u * H // 2, number * H + (u + 1) * H // 2)
-                quantize(w_codes[:, cols], w_scales[:, cols], w_bf[number][u][:].rearrange("p t m j -> p (t m) j"))
+        stationary = [w_codes[:, n * P : (n + 1) * P] for n in range(6)]
+
+        def quantize_w2(u, codes):
+            cols = slice(H + u * H // 2, H + (u + 1) * H // 2)
+            quantize(codes, w_scales[:, cols], w_bf[1][:, 2 * u : 2 * u + 2].rearrange("p t m j -> p (t m) j"))
 
         def second(acc, number, t, codes, scales, start, stop):
-            m = slice(number * H + t * P, number * H + (t + 1) * P)
-            multiply(acc, w_codes[:, m], w_scales[:, m], codes, scales, start, stop)
+            n = number * PACK + t
+            multiply(acc, stationary[n], w_scales[:, n * P : (n + 1) * P], codes, scales, start, stop)
 
         def fetch_all(name, offsets, width, factor=1.0, tag=None):
             found = sbuf(name, [P, PACK, width], F32, tag=tag)
             for t in range(PACK):
                 fetch(found[:, t, :], h[t][:], offsets, factor)
             return found
-
-        def add_all(total, offsets, earlier):
-            for t in range(PACK):
-                nc.vector.tensor_tensor(total[:, t, :], h[t][:].indirect(offsets), earlier[:, t, :], ADD)
 
         def join(z_bf, left, right):
             nc.vector.tensor_tensor(
@@ -201,64 +208,79 @@ def tile_picked_sagecat_mean_lo_kernel(
         def quantize_w3(e):
             for t in range(PACK):
                 cols = slice(t * P + e * P // 2, t * P + (e + 1) * P // 2)
-                quantize(w_codes[:, cols], w_scales[:, cols], w_bf[0][t // 2][:, t % 2, e * P // 2 : (e + 1) * P // 2, :])
+                quantize(w_codes[:, cols], w_scales[:, cols], w_bf[0][:, t, e * P // 2 : (e + 1) * P // 2, :])
 
         quantize_w3(0)
         round_weights(0, 1)
-        one = fetch_all("one", lists[0][:], V)
         quantize_w3(1)
-        two = rows_sb[:, 3:16:4, :]
+        two = [place("two%d" % t, [P, V], F32, kib) for t, kib in enumerate((0, 1, 12, 13))]
         for t in range(PACK):
-            if t == 1:
-                round_weights(1, 0)
             if t == 2:
+                round_weights(1, 0)
                 round_weights(1, 1)
-                quantize_weights(1)
-            nc.vector.tensor_tensor(two[:, t, :], h[t][:].indirect(lists[1][:]), one[:, t, :], ADD)
-        three = fetch_all("three", lists[2][:], V, tag="w_raw0")
-        four = sbuf("four", [P, 2, PACK, HV], F32, tag="w_bf1_1")
-        add_all(four[:, 0], half_of(lists[3], 0, HV), three[:, :, 0:HV])
-        centres = fetch_all("centres0", half_of(cen_sb, 0, HV), HV, 4.0, tag="w1_scales3")
-        zg_bf = sbuf("zg_bf", [P, 2, HV, PACK], BF16)
-        nc.scalar.copy(woven(zg_bf[:, 1]), planes(centres[:]))
-        join(zg_bf[:, 0], two[:, :, 0:HV], four[:, 0])
-        zg_codes = sbuf("zg_codes", [P, V], U32)
-        zg_scales = sbuf("zg_scales", [P, V], U8)
-        quantize(zg_codes[:], zg_scales[:], zg_bf[:].rearrange("p n c t -> p (n c) t"))
-        whole = bank(5, "y_acc", [P, PACK, HV])
+            if t == 3:
+                quantize_w2(0, w_codes[:, H : H + H // 2])
+            nc.vector.tensor_tensor(two[t][:], h[t][:].indirect(lists[1][:]), one[:, t, :], ADD)
+        centres = fetch_all("centres", cen_sb[:], V, 4.0, tag="w_raw0")
+        three = fetch_all("three", third_sb[:], V)
+        four = place("four", [P, PACK, V], F32, 14)
+        g_bf = place("g_bf", [P, V, PACK], BF16, 1)[:]
+        g_codes = sbuf("g_codes", [P, V], U32)
+        g_scales = sbuf("g_scales", [P, V], U8)
+        z_codes = sbuf("z_codes", [P, V], U32)
+        z_scales = sbuf("z_scales", [P, V], U8)
+        halves = [slice(0, HV), slice(HV, V)]
+        first_pairs = [bank(5, "y_first_acc0", [P, 2, HV]), bank(1, "y_first_acc1", [P, 2, HV])]
+        first_acc = [first_pairs[t // 2][:, t % 2, :] for t in range(PACK)]
+        last_pair = bank(6, "y_acc_pair", [P, 2, HV])
+        accs = [bank(7, "y_acc0", [P, HV])[:], bank(0, "y_acc1", [P, HV])[:], last_pair[:, 0, :], last_pair[:, 1, :]]
         for t in range(PACK):
-            for number in range(2):
-                cols = slice(number * HV, (number + 1) * HV)
-                second(whole[:, t, :], number, t, zg_codes[:, cols], zg_scales[:, cols], number == 0, number == 1)
+            nc.vector.tensor_tensor(four[:, t, :], h[t][:].indirect(fourth_sb[:]), two[t][:], ADD)
+            if t == 1:
+                nc.vector.tensor_copy(woven(g_bf), planes(centres[:]))
+            if t == 2:
+                quantize(g_codes[:], g_scales[:], g_bf)
+                for u in range(2):
+                    second(first_acc[u], 1, u, g_codes[:, halves[0]], g_scales[:, halves[0]], u == 0, False)
+                    second(accs[u], 1, u, g_codes[:, halves[1]], g_scales[:, halves[1]], True, False)
+        last_codes = place("w2_last_codes", [P, H // 2], U32, 13)
+        quantize_w2(1, last_codes[:])
+        stationary.extend([last_codes[:, 0:P], last_codes[:, P : 2 * P]])
+        for t in range(2, PACK):
+            second(first_acc[t], 1, t, g_codes[:, halves[0]], g_scales[:, halves[0]], t == 2, False)
+            second(accs[t], 1, t, g_codes[:, halves[1]], g_scales[:, halves[1]], t == 2, False)
 
-        add_all(four[:, 1], half_of(lists[3], 1, HV), three[:, :, HV:V])
-        centres = fetch_all("centres1", half_of(cen_sb, 1, HV), HV, 4.0, tag="x_scales")
-        z_bf = sbuf("z_bf", [P, HV, PACK], BF16)
-        join(z_bf[:], two[:, :, HV:V], four[:, 1])
-        g_bf = sbuf("g_bf", [P, HV, PACK], BF16, tag="zg_bf")
-        nc.vector.tensor_copy(woven(g_bf[:]), planes(centres[:]))
-        z_codes = sbuf("z_codes", [P, HV], U32)
-        z_scales = sbuf("z_scales", [P, HV], U8)
-        quantize(z_codes[:], z_scales[:], z_bf[:])
-        g_codes = sbuf("g_codes", [P, HV], U32)
-        g_scales = sbuf("g_scales", [P, HV], U8)
-        quantize(g_codes[:], g_scales[:], g_bf[:])
+        runs = [slice(0, HV), slice(HV, HV + HV // 2), slice(HV + HV // 2, V)]
+        y_first = sbuf("y_first", [P, PACK, HV], F32)
+        z_bf = [sbuf("z_bf%d" % n, [P, runs[n].stop - runs[n].start, PACK], BF16)[:] for n in range(2)]
+        z_bf.append(y_first[:, 0, :].bitcast(BF16).rearrange("p (c t) -> p c t", t=PACK))
 
-        y_first = sbuf("y_first", [P, PACK, HV], F32, tag="x_scales")
-        nc.scalar.copy(y_first[:], whole[:])
+        def join_run(n):
+            join(z_bf[n], four[:, :, runs[n]], three[:, :, runs[n]])
+
+        def quantize_run(n):
+            quantize(z_codes[:, runs[n]], z_scales[:, runs[n]], z_bf[n])
+
+        join_run(0)
+        join_run(1)
+        quantize_run(0)
+        for t in range(PACK):
+            second(first_acc[t], 0, t, z_codes[:, halves[0]], z_scales[:, halves[0]], False, t % 2 == 1)
+        join_run(2)
+        quantize_run(1)
+        quantize_run(2)
+
+        nc.vector.tensor_copy(y_first[:, 0:2, :], first_pairs[0][:])
+        nc.scalar.copy(y_first[:, 2:4, :], first_pairs[1][:])
         nc.sync.dma_start(out_rows[:, :, 0:HV], y_first[:])
-        y_first_bf = sbuf("y_first_bf", [P, HV, PACK], BF16, tag="zg_bf")
+        y_first_bf = sbuf("y_first_bf", [P, HV, PACK], BF16)
         nc.vector.tensor_copy(woven(y_first_bf[:]), planes(y_first[:]))
         hand_out(0, y_first_bf)
 
         y_second = sbuf("y_second", [P, PACK, HV], F32)
         y_second_bf = sbuf("y_second_bf", [P, HV, PACK], BF16)
-        last_pair = bank(6, "y_acc_pair", [P, 2, HV])
-        accs = [bank(7, "y_acc0", [P, HV])[:], bank(0, "y_acc1", [P, HV])[:], last_pair[:, 0, :], last_pair[:, 1, :]]
         for t in range(PACK):
-            second(accs[t], 0, t, z_codes[:], z_scales[:], t != 3, False)
-        for t in range(PACK):
-            second(accs[t], 1, t, g_codes[:], g_scales[:], False, t != 2)
+            second(accs[t], 0, t, z_codes[:, halves[1]], z_scales[:, halves[1]], False, t != 2)
         for t in range(2):
             nc.scalar.copy(y_second[:, t, :], accs[t])
         nc.sync.dma_start(out_rows[:, 0:2, HV:V], y_second[:, 0:2, :])

from contextlib import ExitStack

import concourse.mybir as mybir

K, T, S, V, H = 512, 1024, 512, 256, 512
FLOPS = 2 * K * H * S + 2 * 2 * H * H * V

F32 = mybir.dt.float32
BF16 = mybir.dt.bfloat16
I32 = mybir.dt.int32
U32 = mybir.dt.uint32
U16 = mybir.dt.uint16
U8 = mybir.dt.uint8
FP8X4 = mybir.dt.float8_e4m3fn_x4
ADD = mybir.AluOpType.add
COPY = mybir.ActivationFunctionType.Copy
RELU = mybir.ActivationFunctionType.Relu

P = 128
PACK = 4
HS = S // 2
HV = V // 2


def tile_picked_sagecat_mean_lo_kernel(
    tc, xT, w1, w2, w3, offs, cen, pos1, pos2, pos3, pos4, out_0, out_1, out_2
):
    nc = tc.nc

    def woven(ap):
        return ap.rearrange("p (c i) t -> p c t i", i=4)

    def planes(ap):
        return ap.rearrange("p t (c i) -> p c t i", i=4)

    def quantize(codes, scales, values):
        nc.vector.quantize_mx(out=codes.bitcast(FP8X4), scales=scales, in_=values.rearrange("p c t -> p (c t)"))

    def multiply(acc, w_codes, w_scales, a_codes, a_scales, start, stop):
        nc.tensor.matmul_mx(
            out=acc,
            lhsT=w_codes.bitcast(FP8X4),
            lhsT_scale=w_scales,
            rhs=a_codes.bitcast(FP8X4),
            rhs_scale=a_scales,
            start=start,
            stop=stop,
        )

    with ExitStack() as ctx:
        sb = ctx.enter_context(tc.tile_pool(name="sb", bufs=1))
        placed = ctx.enter_context(tc.tile_pool(name="placed", bufs=1))
        psum = ctx.enter_context(tc.psum_pool(name="psum", bufs=1))

        def sbuf(name, shape, dtype, tag=None):
            return sb.tile(shape, dtype, name=name, tag=tag or name, align_bytes=256)

        def place(name, shape, dtype, kib):
            return placed.tile(shape, dtype, name=name, align_bytes=256, offset=kib * 1024)

        def bank(number, name, shape):
            return psum.tile(shape, F32, name=name, tag="bank%d" % number)

        offs_sb = sb.tile([P, S // 16], U16, name="offs_sb")
        x_rows = xT.rearrange("(p j) n -> p j n", j=PACK)
        x_raw = [sbuf("x_raw%d" % j, [P, T], F32) for j in range(PACK)]
        for j in range(PACK):
            nc.sync.dma_start(x_raw[j][:], x_rows[:, j, :])
            if j == 0:
                nc.sync.dma_start(offs_sb[:], offs)
        w1_raw = sbuf("w1_raw", [P, PACK, H], F32)
        nc.sync.dma_start(w1_raw[:], w1.rearrange("(p j) c -> p j c", j=PACK))
        lists = []

        def load_lists(sources):
            for src in sources:
                list_sb = sb.tile([P, V // 16], U16, name="list%d" % len(lists))
                nc.sync.dma_start(list_sb[:], src)
                lists.append(list_sb)

        load_lists([pos1])
        w_raw = [sbuf("w_raw0", [P, PACK, H // 2], F32)[:]]
        w_raw.extend([place("w_raw%d" % n, [P, PACK, H // 2], F32, kib)[:] for n, kib in ((1, 0), (2, 4), (3, 12))])
        for number, w in enumerate((w3, w2)):
            if number == 1:
                load_lists([pos2, cen])
            rows = w.rearrange("(p j) c -> p j c", j=PACK)
            for e in range(2):
                nc.sync.dma_start(w_raw[2 * number + e], rows[:, :, e * H // 2 : (e + 1) * H // 2])
        load_lists([pos4, pos3])
        cen_sb, fourth_sb, third_sb = lists[2:5]

        def half_of(list_sb, half, entries):
            return list_sb[:, half * entries // 16 : (half + 1) * entries // 16]

        def fetch(out, window, offsets, factor=1.0):
            nc.scalar.activation(out, window.indirect(offsets), COPY, scale=factor)

        x_codes = sbuf("x_codes", [P, S], U32)
        x_scales = sbuf("x_scales", [P, S], U8)
        x_bf = [sbuf("x_bf%d" % a, [P, HS, PACK], BF16) for a in range(2)]
        x_found = [sbuf("x_found%d" % a, [P, PACK, HS], F32) for a in range(2)]
        for j in range(PACK):
            if j < PACK - 1:
                nc.vector.tensor_copy(x_found[0][:, j, :], x_raw[j][:].indirect(half_of(offs_sb, 0, HS)))
            else:
                for q in range(2):
                    nc.vector.tensor_copy(x_found[0][:, j, q * P : (q + 1) * P], x_raw[j][:].indirect(half_of(offs_sb, q, P)))
            if j < 2:
                nc.vector.tensor_copy(x_found[1][:, j, 0:P], x_raw[j][:].indirect(half_of(offs_sb, 2, P)))
                fetch(x_found[1][:, j, P:HS], x_raw[j][:], half_of(offs_sb, 3, P))
            elif j == 2:
                fetch(x_found[1][:, j, :], x_raw[j][:], half_of(offs_sb, 1, HS))
            else:
                for q in range(2):
                    fetch(x_found[1][:, j, q * P : (q + 1) * P], x_raw[j][:], half_of(offs_sb, 2 + q, P))
        for first, last, weave, a in (
            (0, 128, nc.scalar.copy, 1),
            (128, 192, nc.scalar.copy, 1),
            (0, 128, nc.vector.tensor_copy, 0),
            (128, 256, nc.vector.tensor_copy, 0),
            (192, 256, nc.vector.tensor_copy, 1),
        ):
            weave(woven(x_bf[a][:, first:last, :]), planes(x_found[a][:, :, first:last]))
        for a in range(2):
            cols = slice(a * HS, (a + 1) * HS)
            quantize(x_codes[:, cols], x_scales[:, cols], x_bf[a][:])

        w1_dealt = w1_raw[:].rearrange("p j (m u t) -> p u m j t", u=2, t=2)
        h = [sbuf("h%d" % t, [P, S], F32) for t in range(PACK)]
        w1_bf = []
        for u in range(2):
            rounded = sbuf("w1_bf%d" % u, [P, 2, P, PACK], BF16)
            dealt = rounded[:].rearrange("p t m j -> p m j t")
            share = (80, 32)[u]
            nc.vector.tensor_copy(dealt[:, 0:share], w1_dealt[:, u, 0:share])
            nc.scalar.copy(dealt[:, share:P], w1_dealt[:, u, share:P])
            w1_bf.extend([rounded[:, 0], rounded[:, 1]])
        w_bf = [sbuf("w_bf%d" % number, [P, PACK, P, PACK], BF16) for number in range(2)]

        def round_weights(number, e):
            src = w_raw[2 * number + e].rearrange("p j (m u t) -> p u m j t", u=2, t=2)
            dst = w_bf[number][:].rearrange("p (u t) (e m) j -> p e u m j t", u=2, e=2)[:, e]
            if (number, e) == (0, 1):
                for u in range(2):
                    nc.vector.tensor_copy(dst[:, u], src[:, u])
            else:
                nc.vector.tensor_copy(dst, src)

        one = sbuf("one", [P, PACK, V], F32)
        pair_codes = []
        for t in range(PACK):
            if t == 2:
                round_weights(0, 0)
            if t % 2 == 0:
                pair_codes.append(sbuf("w1_codes%d" % (t + 1), [P, 2, P], U32, tag="w_raw0" if t == 2 else None))
            w1_codes = pair_codes[t // 2][:, t % 2]
            w1_scales = sbuf("w1_scales%d" % t, [P, P], U8)
            quantize(w1_codes, w1_scales[:], w1_bf[t])
            if t == 0:
                for a in range(2):
                    cols = slice(a * HS, (a + 1) * HS)
                    acc = bank(a, "h0_acc%d" % a, [P, HS])
                    multiply(acc[:], w1_codes, w1_scales[:], x_codes[:, cols], x_scales[:, cols], True, True)
                    nc.scalar.activation(h[0][:, cols], acc[:], RELU, scale=0.25)
            else:
                acc = bank(1 + t, "h_acc%d" % t, [P, S])
                multiply(acc[:], w1_codes, w1_scales[:], x_codes[:], x_scales[:], True, True)
                nc.scalar.activation(h[t][:], acc[:], RELU, scale=0.25)
            fetch(one[:, t, :], h[t][:], lists[0][:])

        w_codes = sbuf("w_codes", [P, H + H // 2], U32)
        w_scales = sbuf("w_scales", [P, 2 * H], U8)

        stationary = [w_codes[:, n * P : (n + 1) * P] for n in range(6)]

        def quantize_w2(u, codes):
            cols = slice(H + u * H // 2, H + (u + 1) * H // 2)
            quantize(codes, w_scales[:, cols], w_bf[1][:, 2 * u : 2 * u + 2].rearrange("p t m j -> p (t m) j"))

        def second(acc, number, t, codes, scales, start, stop):
            n = number * PACK + t
            multiply(acc, stationary[n], w_scales[:, n * P : (n + 1) * P], codes, scales, start, stop)

        def fetch_all(name, offsets, width, factor=1.0, tag=None):
            found = sbuf(name, [P, PACK, width], F32, tag=tag)
            for t in range(PACK):
                fetch(found[:, t, :], h[t][:], offsets, factor)
            return found

        def join(z_bf, left, right):
            nc.vector.tensor_tensor(
                woven(z_bf),
                planes(left),
                planes(right),
                ADD,
            )

        y_codes = sbuf("y_codes", [P, V], U32)
        y_scales = sbuf("y_scales", [P, V], U8)
        out_rows = out_0.rearrange("(p t) v -> p t v", t=PACK)
        out_words = out_1[0].rearrange("p c r -> p (c r)").bitcast(I32)

        def hand_out(a, y_bf):
            cols = slice(a * HV, (a + 1) * HV)
            quantize(y_codes[:, cols], y_scales[:, cols], y_bf[:])

        def quantize_w3(e):
            for t in range(PACK):
                cols = slice(t * P + e * P // 2, t * P + (e + 1) * P // 2)
                quantize(w_codes[:, cols], w_scales[:, cols], w_bf[0][:, t, e * P // 2 : (e + 1) * P // 2, :])

        quantize_w3(0)
        round_weights(0, 1)
        quantize_w3(1)
        two = [place("two%d" % t, [P, V], F32, kib) for t, kib in enumerate((0, 1, 12, 13))]
        for t in range(PACK):
            if t == 2:
                round_weights(1, 0)
                round_weights(1, 1)
            if t == 3:
                quantize_w2(0, w_codes[:, H : H + H // 2])
            nc.vector.tensor_tensor(two[t][:], h[t][:].indirect(lists[1][:]), one[:, t, :], ADD)
        centres = fetch_all("centres", cen_sb[:], V, 4.0, tag="w_raw0")
        three = fetch_all("three", third_sb[:], V)
        four = place("four", [P, PACK, V], F32, 14)
        g_bf = place("g_bf", [P, V, PACK], BF16, 1)[:]
        g_codes = sbuf("g_codes", [P, V], U32)
        g_scales = sbuf("g_scales", [P, V], U8)
        z_codes = sbuf("z_codes", [P, V], U32)
        z_scales = sbuf("z_scales", [P, V], U8)
        halves = [slice(0, HV), slice(HV, V)]
        first_pairs = [bank(5, "y_first_acc0", [P, 2, HV]), bank(1, "y_first_acc1", [P, 2, HV])]
        first_acc = [first_pairs[t // 2][:, t % 2, :] for t in range(PACK)]
        last_pair = bank(6, "y_acc_pair", [P, 2, HV])
        accs = [bank(7, "y_acc0", [P, HV])[:], bank(0, "y_acc1", [P, HV])[:], last_pair[:, 0, :], last_pair[:, 1, :]]
        for t in range(PACK):
            nc.vector.tensor_tensor(four[:, t, :], h[t][:].indirect(fourth_sb[:]), two[t][:], ADD)
            if t == 1:
                nc.vector.tensor_copy(woven(g_bf), planes(centres[:]))
            if t == 2:
                quantize(g_codes[:], g_scales[:], g_bf)
                for u in range(2):
                    second(first_acc[u], 1, u, g_codes[:, halves[0]], g_scales[:, halves[0]], u == 0, False)
                    second(accs[u], 1, u, g_codes[:, halves[1]], g_scales[:, halves[1]], True, False)
        last_codes = place("w2_last_codes", [P, H // 2], U32, 13)
        quantize_w2(1, last_codes[:])
        stationary.extend([last_codes[:, 0:P], last_codes[:, P : 2 * P]])
        for t in range(2, PACK):
            second(first_acc[t], 1, t, g_codes[:, halves[0]], g_scales[:, halves[0]], t == 2, False)
            second(accs[t], 1, t, g_codes[:, halves[1]], g_scales[:, halves[1]], t == 2, False)

        runs = [slice(0, HV), slice(HV, HV + HV // 2), slice(HV + HV // 2, V)]
        y_first = sbuf("y_first", [P, PACK, HV], F32)
        z_bf = [sbuf("z_bf%d" % n, [P, runs[n].stop - runs[n].start, PACK], BF16)[:] for n in range(2)]
        z_bf.append(y_first[:, 0, :].bitcast(BF16).rearrange("p (c t) -> p c t", t=PACK))

        def join_run(n):
            join(z_bf[n], four[:, :, runs[n]], three[:, :, runs[n]])

        def quantize_run(n):
            quantize(z_codes[:, runs[n]], z_scales[:, runs[n]], z_bf[n])

        join_run(0)
        join_run(1)
        quantize_run(0)
        for t in range(PACK):
            second(first_acc[t], 0, t, z_codes[:, halves[0]], z_scales[:, halves[0]], False, t % 2 == 1)
        join_run(2)
        quantize_run(1)
        quantize_run(2)

        nc.vector.tensor_copy(y_first[:, 0:2, :], first_pairs[0][:])
        nc.scalar.copy(y_first[:, 2:4, :], first_pairs[1][:])
        nc.sync.dma_start(out_rows[:, :, 0:HV], y_first[:])
        y_first_bf = sbuf("y_first_bf", [P, HV, PACK], BF16)
        nc.vector.tensor_copy(woven(y_first_bf[:]), planes(y_first[:]))
        hand_out(0, y_first_bf)

        y_second = sbuf("y_second", [P, PACK, HV], F32)
        y_second_bf = sbuf("y_second_bf", [P, HV, PACK], BF16)
        for t in range(PACK):
            second(accs[t], 0, t, z_codes[:, halves[1]], z_scales[:, halves[1]], False, t != 2)
        for t in range(2):
            nc.scalar.copy(y_second[:, t, :], accs[t])
        nc.sync.dma_start(out_rows[:, 0:2, HV:V], y_second[:, 0:2, :])
        nc.vector.tensor_copy(y_second_bf[:, :, 0:2], y_second[:, 0:2, :].rearrange("p t v -> p v t"))
        nc.scalar.copy(y_second_bf[:, :, 2:4], last_pair[:].rearrange("p t v -> p v t"))
        nc.scalar.copy(y_second[:, 2:4, :], last_pair[:])
        nc.scalar.dma_start(out_rows[:, 2:4, HV:V], y_second[:, 2:4, :])
        hand_out(1, y_second_bf)

        nc.sync.dma_start(out_words, y_codes[:].bitcast(I32))
        for q in range(4):
            queue = nc.scalar if q >= 2 else nc.sync
            queue.dma_start(out_2[0, 4 * q : 4 * q + 4, :].bitcast(I32), y_scales[32 * q : 32 * q + 4, :].bitcast(I32))
